import numpy as np
import ml_dtypes


def mxq(x, axis, fmt="e4m3"):
    dtype, down = {"e4m3": (ml_dtypes.float8_e4m3fn, 7), "e5m2": (ml_dtypes.float8_e5m2, 14)}[fmt]
    v = np.moveaxis(np.asarray(x, np.float32).astype(ml_dtypes.bfloat16).astype(np.float64), axis, -1)
    blocks = v.reshape(v.shape[:-1] + (-1, 32))
    amax = np.abs(blocks).max(-1, keepdims=True)
    byte = np.maximum(np.where(amax > 0, np.frexp(amax)[1] - 1 + 127, 0) - down, 1)
    scale = np.exp2(byte - 127.0)
    codes = (blocks / scale).astype(np.float32).astype(dtype).astype(np.float64)
    return np.moveaxis((codes * scale).reshape(v.shape), -1, axis)


WIDE = False


def mx_kscale(k):
    if not WIDE:
        return np.ones(k)
    levels = np.array([18, -18])
    if k % 512:
        return np.exp2(np.random.permutation(np.resize(levels, k // 32))).repeat(32)
    a = np.empty((k // 512, 16))
    for p in range(k // 512):
        a[p, :8] = np.random.permutation(np.resize(levels, 8))
        for g in range(8):
            far = levels[np.abs(levels - a[p, g]) >= 10]
            a[p, g + 8] = far[np.random.randint(len(far))]
    return np.exp2(a.ravel()).repeat(32)


def f64(x):
    return np.asarray(x).astype(np.float64)


def striped(idx):
    return np.tile(np.asarray(idx).reshape(-1, 16).T, (8, 1)).astype(np.uint16)


def unstriped(offs):
    return offs[:16].T.reshape(-1).astype(np.int64)

def planes(y):
    n, m = y.shape
    v = y.astype(np.float32).astype(ml_dtypes.bfloat16).astype(np.float64).reshape(n // 32, 32, m)
    top = np.abs(v).max(1)
    byte = np.clip(np.where(top > 0, np.frexp(top)[1] - 1 + 127 - 7, 1), 1, 254)
    codes = (v * np.exp2(127.0 - byte)[:, None, :]).reshape(n, m).astype(np.float32).astype(ml_dtypes.float8_e4m3fn).view(np.uint8)
    words = codes.reshape(n // 512, 128, 4, m).transpose(0, 1, 3, 2)
    return np.ascontiguousarray(words), np.ascontiguousarray(byte.astype(np.uint8).reshape(n // 512, 16, m))


def clip(x, c):
    return np.minimum(np.maximum(x, -c), c)


def setup_inputs():
    n = np.random.standard_normal
    uni = np.random.uniform
    idx = np.random.permutation(2048)[:512]
    f_r = mx_kscale(512)
    return {
        "xT": (n((512, 512)) * f_r[None, :]).astype(np.float32),
        "G": (n((512, 512)) / np.sqrt(512) / f_r[:, None]).astype(np.float32),
        "mT": (n((512, 2048))).astype(np.float32),
        "hT": (uni(0.1, 2.0, (512, 2048))).astype(np.float32),
        "offs": striped(idx),
    }


def reference(xT, G, mT, hT, offs):
    idx = unstriped(offs)
    m = f64(mT)[:, idx]
    h = f64(hT)[:, idx]
    dw = mxq(f64(xT), 1, "e4m3") @ mxq(f64(G), 0, "e5m2")
    nm = 0.9 * m + dw
    up = clip(nm / (h + 0.001), 1.0)
    out_0 = np.zeros((512, 2048))
    out_0[:, idx] = up
    out_1 = np.zeros((512, 2048))
    out_1[:, idx] = nm
    return (out_0, out_1,) + planes(out_0)

@@ -1,0 +1,236 @@
+from contextlib import ExitStack
+
+import concourse.mybir as mybir
+from concourse.masks import make_identity
+
+F32 = mybir.dt.float32
+BF16 = mybir.dt.bfloat16
+U32 = mybir.dt.uint32
+I32 = mybir.dt.int32
+U16 = mybir.dt.uint16
+U8 = mybir.dt.uint8
+E4M3 = mybir.dt.float8_e4m3fn_x4
+E5M2 = mybir.dt.float8_e5m2_x4
+ALU = mybir.AluOpType
+ACT = mybir.ActivationFunctionType
+
+P = 128
+LANES = 4
+D = 512
+R = 512
+SLOTS = 512
+COLS = 2048
+CHUNK = 512
+G_SPLIT = 320
+DECAY = 0.9
+EPS = 0.001
+
+FLOPS = 2 * D * R * SLOTS
+
+
+def tile_attend_gsophia_pl_kernel(tc, xT, G, mT, hT, offs, out_0, out_1, out_2, out_3):
+    nc = tc.nc
+    with ExitStack() as ctx:
+        sb = ctx.enter_context(tc.tile_pool(name="sb", bufs=1))
+        ps = ctx.enter_context(tc.psum_pool(name="ps", bufs=1))
+
+        def tile(name, shape, dtype, tag=None):
+            return sb.tile(shape, dtype, name=name, tag=tag or name, align_bytes=64)
+
+        x_rows = xT.rearrange("(m t) r -> m t r", t=LANES)
+        m_rows = mT.rearrange("(p t) c -> t p c", t=LANES)
+        h_rows = hT.rearrange("(p t) c -> t p c", t=LANES)
+        up_rows = out_0.rearrange("(p t) c -> t p c", t=LANES)
+        nm_rows = out_1.rearrange("(p t) c -> t p c", t=LANES)
+
+        x_first = tile("x_first", [P, R], F32)
+        nc.sync.dma_start(out=x_first[:], in_=x_rows[:, 0, :])
+        g_raw = tile("g_raw", [P, LANES, SLOTS], F32)
+        nc.sync.dma_start(out=g_raw[:], in_=G.rearrange("(p j) w -> p j w", j=LANES))
+        offsets = sb.tile([P, SLOTS // 16], U16, name="offsets")
+        nc.sync.dma_start(offsets[:], offs)
+        m_tab = [tile("m_tab%d" % t, [P, COLS], F32) for t in range(LANES)]
+        h_tab = [tile("h_tab%d" % t, [P, COLS], F32) for t in range(LANES)]
+        nc.sync.dma_start(out=m_tab[0][:], in_=m_rows[0])
+        x_rest = tile("x_rest", [P, LANES - 1, R], F32)
+        nc.sync.dma_start(out=x_rest[:], in_=x_rows[:, 1:LANES, :])
+        nc.sync.dma_start(out=h_tab[0][:], in_=h_rows[0])
+        for t in range(1, LANES):
+            nc.sync.dma_start(out=h_tab[t][:], in_=h_rows[t])
+            nc.sync.dma_start(out=m_tab[t][:], in_=m_rows[t])
+
+        ident = tile("ident", [P, P], F32)
+        make_identity(nc, ident[:])
+
+        up_win = {}
+        nm_win = {}
+        for t in range(2):
+            nm_win[t] = tile("nm_win%d" % t, [P, COLS], F32)
+            nc.vector.memset(nm_win[t][:], 0.0)
+            up_win[t] = tile("up_win%d" % t, [P, COLS], F32)
+            nc.vector.memset(up_win[t][:], 0.0)
+        decay = tile("decay", [P, SLOTS], F32)
+        nc.vector.tensor_scalar(decay[:], nm_win[0][:, 0:SLOTS], 1.0, DECAY, ALU.mult, ALU.add)
+
+        x_codes = tile("x_codes", [P, D], U32)
+        x_scales = tile("x_scales", [P, D], U8)
+
+        def turn_x(t):
+            src = x_first[:] if t == 0 else x_rest[:, t - 1, :]
+            x_bf = tile("x_bf%d" % t, [P, R], BF16)
+            nc.scalar.copy(x_bf[:], src)
+            words = x_bf[:].bitcast(F32)
+            turned = ps.tile([P, 2, P], F32, name="turned%d" % t)
+            for u in range(2):
+                nc.tensor.transpose(turned[:, u, :], words[:, u : R // 2 : 2], ident[:])
+            grouped = tile("x_grouped%d" % t, [P, P * LANES], BF16)
+            nc.scalar.copy(
+                grouped[:].bitcast(F32).rearrange("p (m u) -> p m u", u=2),
+                turned[:].rearrange("p u m -> p m u"),
+            )
+            return grouped
+
+        def quantise_x(t, grouped):
+            cols = slice(t * P, (t + 1) * P)
+            nc.vector.quantize_mx(out=x_codes[:, cols].bitcast(E4M3), scales=x_scales[:, cols], in_=grouped[:])
+
+        quantise_x(0, turn_x(0))
+
+        g_grouped = tile("g_grouped", [P, SLOTS, LANES], BF16)
+        nc.vector.tensor_copy(
+            g_grouped[:, 0:G_SPLIT, :].rearrange("p (c i) j -> p c j i", i=4),
+            g_raw[:, :, 0:G_SPLIT].rearrange("p j (c i) -> p c j i", i=4),
+        )
+        nc.scalar.copy(
+            g_grouped[:, G_SPLIT:SLOTS, :].rearrange("p (c i) j -> p c j i", i=4),
+            g_raw[:, :, G_SPLIT:SLOTS].rearrange("p j (c i) -> p c j i", i=4),
+        )
+        g_codes = tile("g_codes", [P, SLOTS], U32)
+        g_scales = tile("g_scales", [P, SLOTS], U8)
+        nc.vector.quantize_mx(
+            out=g_codes[:].bitcast(E5M2), scales=g_scales[:], in_=g_grouped[:].rearrange("p w j -> p (w j)")
+        )
+
+        def gradient(t):
+            cols = slice(t * P, (t + 1) * P)
+            acc = ps.tile([P, SLOTS], F32, name="acc%d" % t)
+            nc.tensor.matmul_mx(
+                out=acc[:],
+                lhsT=x_codes[:, cols].bitcast(E4M3),
+                lhsT_scale=x_scales[:, cols],
+                rhs=g_codes[:].bitcast(E5M2),
+                rhs_scale=g_scales[:],
+                start=True,
+                stop=True,
+            )
+            dw = tile("dw%d" % t, [P, SLOTS], F32)
+            nc.scalar.activation(dw[:], acc[:], ACT.Copy, scale=1.0 / DECAY)
+            return dw
+
+        def gather_m(t, dw):
+            total = tile("total%d" % t, [P, SLOTS], F32)
+            nc.vector.tensor_tensor(total[:], m_tab[t][:].indirect(offsets[:]), dw[:], ALU.add)
+            return total
+
+        def gather_h(t):
+            h = tile("h%d" % t, [P, SLOTS], F32)
+            nc.vector.tensor_copy(h[:], h_tab[t][:].indirect(offsets[:]))
+            root = tile("root%d" % t, [P, SLOTS], F32, tag="root")
+            nc.scalar.activation(root[:], h[:], ACT.Abs_reciprocal_sqrt, scale=1.0 / DECAY, bias=EPS / DECAY)
+            inv = tile("inv%d" % t, [P, SLOTS], F32)
+            nc.scalar.activation(inv[:], root[:], ACT.Square)
+            sign = tile("sign%d" % t, [P, SLOTS], F32)
+            nc.scalar.activation(sign[:], h[:], ACT.Sign, bias=EPS)
+            return inv, sign
+
+        def late_window(name, tag):
+            win = tile(name, [P, COLS], F32, tag=tag)
+            nc.gpsimd.memset(win[:], 0.0)
+            return win
+
+        def scatter_nm(t, total):
+            nc.vector.tensor_tensor(nm_win[t][:].indirect(offsets[:]), total[:], decay[:], ALU.mult)
+            nc.sync.dma_start(out=nm_rows[t], in_=nm_win[t][:])
+
+        n_chunks = COLS // CHUNK
+        pairs = []
+
+        def ratio(t, total, inv):
+            q = tile("ratio%d" % t, [P, SLOTS], F32, tag="h_tab%d" % ((t + 1) % LANES))
+            nc.vector.tensor_tensor(q[:], total[:], inv[:], ALU.mult)
+            cut = tile("cut%d" % t, [P, SLOTS], F32, tag="m_tab0" if t == LANES - 1 else None)
+            nc.vector.tensor_scalar(cut[:], q[:], 1.0, -1.0, ALU.min, ALU.max)
+            return cut
+
+        def scatter_up(t, cut, sign):
+            nc.vector.tensor_tensor(up_win[t][:].indirect(offsets[:]), cut[:], sign[:], ALU.mult)
+            nc.sync.dma_start(out=up_rows[t], in_=up_win[t][:])
+
+        def round_up(t, c):
+            nc.scalar.copy(pairs[c][:, t // 2, :, t % 2], up_win[t][:, c * CHUNK : (c + 1) * CHUNK])
+
+        y_scales = tile("y_scales", [P, COLS], U8)
+
+        def weave(c):
+            woven = tile("woven%d" % c, [P, CHUNK * LANES], BF16, tag=("m_tab1", "m_tab2", "m_tab3", "h_tab3")[c])
+            nc.scalar.copy(
+                woven[:].bitcast(U32).rearrange("p (c u) -> p c u", u=2),
+                pairs[c][:].rearrange("p u c e -> p u (c e)").bitcast(U32).rearrange("p u c -> p c u"),
+            )
+            return woven
+
+        def quantise_y(c, woven):
+            cols = slice(c * CHUNK, (c + 1) * CHUNK)
+            codes = tile("y_codes%d" % c, [P, CHUNK], U32)
+            nc.vector.quantize_mx(out=codes[:].bitcast(E4M3), scales=y_scales[:, cols], in_=woven[:])
+            nc.sync.dma_start(
+                out=out_2[0, :, cols, :].rearrange("p c l -> p (c l)").bitcast(I32), in_=codes[:].bitcast(I32)
+            )
+
+        total0 = gather_m(0, gradient(0))
+        scatter_nm(0, total0)
+        for t in range(1, LANES):
+            quantise_x(t, turn_x(t))
+        inv0, sign0 = gather_h(0)
+        dws = {t: gradient(t) for t in range(1, LANES)}
+        for c, tag in enumerate(("g_raw", "x_rest", "g_grouped", "pairs")):
+            pairs.append(tile("pairs%d" % c, [P, 2, CHUNK, 2], BF16, tag=tag))
+        inv1, sign1 = gather_h(1)
+        cut0 = ratio(0, total0, inv0)
+        up_win[2] = late_window("up_win2", "h_tab1")
+        scatter_up(0, cut0, sign0)
+        for c in range(n_chunks):
+            round_up(0, c)
+        total1 = gather_m(1, dws[1])
+        scatter_nm(1, total1)
+        inv2, sign2 = gather_h(2)
+        cut1 = ratio(1, total1, inv1)
+        up_win[3] = late_window("up_win3", "h_tab2")
+        scatter_up(1, cut1, sign1)
+        for c in range(n_chunks):
+            round_up(1, c)
+        total2 = gather_m(2, dws[2])
+        inv3, sign3 = gather_h(3)
+        cut2 = ratio(2, total2, inv2)
+        scatter_up(2, cut2, sign2)
+        for c in range(n_chunks):
+            round_up(2, c)
+        total3 = gather_m(3, dws[3])
+        cut3 = ratio(3, total3, inv3)
+        nm_win[2] = late_window("nm_win2", "h_tab0")
+        scatter_up(3, cut3, sign3)
+        nm_win[3] = late_window("nm_win3", "m_tab0")
+        wovens = []
+        for c in range(n_chunks):
+            round_up(3, c)
+            wovens.append(weave(c))
+        scatter_nm(2, total2)
+        for c in range(2):
+            quantise_y(c, wovens[c])
+        scatter_nm(3, total3)
+        for c in range(2, n_chunks):
+            quantise_y(c, wovens[c])
+        for q in range(4):
+            nc.sync.dma_start(
+                out=out_3[0, 4 * q : 4 * q + 4, :].bitcast(I32), in_=y_scales[32 * q : 32 * q + 4, :].bitcast(I32)
+            )

@@ -21,7 +21,7 @@ R = 512
 SLOTS = 512
 COLS = 2048
 CHUNK = 512
-G_SPLIT = 320
+G_SPLIT = 160
 DECAY = 0.9
 EPS = 0.001
 
@@ -45,8 +45,11 @@ def tile_attend_gsophia_pl_kernel(tc, xT, G, mT, hT, offs, out_0, out_1, out_2, 
 
         x_first = tile("x_first", [P, R], F32)
         nc.sync.dma_start(out=x_first[:], in_=x_rows[:, 0, :])
-        g_raw = tile("g_raw", [P, LANES, SLOTS], F32)
-        nc.sync.dma_start(out=g_raw[:], in_=G.rearrange("(p j) w -> p j w", j=LANES))
+        half = SLOTS // 2
+        g_rows = G.rearrange("(p j) w -> p j w", j=LANES)
+        g_raw = [tile("g_raw%d" % a, [P, LANES, half], F32) for a in range(2)]
+        for a in range(2):
+            nc.sync.dma_start(out=g_raw[a][:], in_=g_rows[:, :, a * half : (a + 1) * half])
         offsets = sb.tile([P, SLOTS // 16], U16, name="offsets")
         nc.sync.dma_start(offsets[:], offs)
         m_tab = [tile("m_tab%d" % t, [P, COLS], F32) for t in range(LANES)]
@@ -55,8 +58,10 @@ def tile_attend_gsophia_pl_kernel(tc, xT, G, mT, hT, offs, out_0, out_1, out_2, 
         x_rest = tile("x_rest", [P, LANES - 1, R], F32)
         nc.sync.dma_start(out=x_rest[:], in_=x_rows[:, 1:LANES, :])
         nc.sync.dma_start(out=h_tab[0][:], in_=h_rows[0])
+        nc.sync.dma_start(out=h_tab[1][:], in_=h_rows[1])
         for t in range(1, LANES):
-            nc.sync.dma_start(out=h_tab[t][:], in_=h_rows[t])
+            if t + 1 < LANES:
+                nc.sync.dma_start(out=h_tab[t + 1][:], in_=h_rows[t + 1])
             nc.sync.dma_start(out=m_tab[t][:], in_=m_rows[t])
 
         ident = tile("ident", [P, P], F32)
@@ -64,60 +69,70 @@ def tile_attend_gsophia_pl_kernel(tc, xT, G, mT, hT, offs, out_0, out_1, out_2, 
 
         up_win = {}
         nm_win = {}
-        for t in range(2):
-            nm_win[t] = tile("nm_win%d" % t, [P, COLS], F32)
-            nc.vector.memset(nm_win[t][:], 0.0)
-            up_win[t] = tile("up_win%d" % t, [P, COLS], F32)
-            nc.vector.memset(up_win[t][:], 0.0)
+        one = tile("one", [P, 1], F32)
+        nc.vector.memset(one[:], 1.0)
+        warm = tile("warm", [P, 1], F32)
+        nc.scalar.activation(warm[:], one[:], ACT.Abs_reciprocal_sqrt)
+
+        def window(name, tag=None):
+            win = tile(name, [P, COLS], F32, tag=tag)
+            nc.vector.memset(win[:].bitcast(I32), 0)
+            return win
+
+        nm_win[0] = window("nm_win0")
+        up_win[0] = window("up_win0")
         decay = tile("decay", [P, SLOTS], F32)
         nc.vector.tensor_scalar(decay[:], nm_win[0][:, 0:SLOTS], 1.0, DECAY, ALU.mult, ALU.add)
 
-        x_codes = tile("x_codes", [P, D], U32)
-        x_scales = tile("x_scales", [P, D], U8)
-
-        def turn_x(t):
-            src = x_first[:] if t == 0 else x_rest[:, t - 1, :]
-            x_bf = tile("x_bf%d" % t, [P, R], BF16)
-            nc.scalar.copy(x_bf[:], src)
+        def quantise_x(name, x_bf, planes, scales):
             words = x_bf[:].bitcast(F32)
-            turned = ps.tile([P, 2, P], F32, name="turned%d" % t)
-            for u in range(2):
-                nc.tensor.transpose(turned[:, u, :], words[:, u : R // 2 : 2], ident[:])
-            grouped = tile("x_grouped%d" % t, [P, P * LANES], BF16)
+            turned = ps.tile([P, len(planes), 2, P], F32, name="turned" + name)
+            for i, t in enumerate(planes):
+                for u in range(2):
+                    nc.tensor.transpose(
+                        turned[:, i, u, :], words[:, t * (R // 2) + u : (t + 1) * (R // 2) : 2], ident[:]
+                    )
+            grouped = tile("x_grouped" + name, [P, len(planes) * P * LANES], BF16)
             nc.scalar.copy(
-                grouped[:].bitcast(F32).rearrange("p (m u) -> p m u", u=2),
-                turned[:].rearrange("p u m -> p m u"),
+                grouped[:].bitcast(F32).rearrange("p (t m u) -> p t m u", u=2, m=P),
+                turned[:].rearrange("p t u m -> p t m u"),
             )
-            return grouped
+            codes = tile("x_codes" + name, [P, len(planes) * P], U32)
+            nc.vector.quantize_mx(out=codes[:].bitcast(E4M3), scales=scales, in_=grouped[:])
+            return [(codes[:, i * P : (i + 1) * P], scales[:, i * P : (i + 1) * P]) for i in range(len(planes))]
 
-        def quantise_x(t, grouped):
-            cols = slice(t * P, (t + 1) * P)
-            nc.vector.quantize_mx(out=x_codes[:, cols].bitcast(E4M3), scales=x_scales[:, cols], in_=grouped[:])
+        x_bf = tile("x_bf", [P, R], BF16)
+        nc.scalar.copy(x_bf[:], x_first[:])
+        x_scales0 = tile("x_scales0", [P, P], U8)
+        x_mx = quantise_x("0", x_bf, [0], x_scales0[:])
 
-        quantise_x(0, turn_x(0))
-
-        g_grouped = tile("g_grouped", [P, SLOTS, LANES], BF16)
-        nc.vector.tensor_copy(
-            g_grouped[:, 0:G_SPLIT, :].rearrange("p (c i) j -> p c j i", i=4),
-            g_raw[:, :, 0:G_SPLIT].rearrange("p j (c i) -> p c j i", i=4),
-        )
-        nc.scalar.copy(
-            g_grouped[:, G_SPLIT:SLOTS, :].rearrange("p (c i) j -> p c j i", i=4),
-            g_raw[:, :, G_SPLIT:SLOTS].rearrange("p j (c i) -> p c j i", i=4),
-        )
         g_codes = tile("g_codes", [P, SLOTS], U32)
         g_scales = tile("g_scales", [P, SLOTS], U8)
-        nc.vector.quantize_mx(
-            out=g_codes[:].bitcast(E5M2), scales=g_scales[:], in_=g_grouped[:].rearrange("p w j -> p (w j)")
-        )
+        for a in range(2):
+            g_grouped = tile("g_grouped%d" % a, [P, half, LANES], BF16)
+            split = half if a == 0 else G_SPLIT
+            nc.vector.tensor_copy(
+                g_grouped[:, 0:split, :].rearrange("p (c i) j -> p c j i", i=4),
+                g_raw[a][:, :, 0:split].rearrange("p j (c i) -> p c j i", i=4),
+            )
+            if split < half:
+                nc.scalar.copy(
+                    g_grouped[:, split:half, :].rearrange("p (c i) j -> p c j i", i=4),
+                    g_raw[a][:, :, split:half].rearrange("p j (c i) -> p c j i", i=4),
+                )
+            cols = slice(a * half, (a + 1) * half)
+            nc.vector.quantize_mx(
+                out=g_codes[:, cols].bitcast(E5M2),
+                scales=g_scales[:, cols],
+                in_=g_grouped[:].rearrange("p w j -> p (w j)"),
+            )
 
         def gradient(t):
-            cols = slice(t * P, (t + 1) * P)
             acc = ps.tile([P, SLOTS], F32, name="acc%d" % t)
             nc.tensor.matmul_mx(
                 out=acc[:],
-                lhsT=x_codes[:, cols].bitcast(E4M3),
-                lhsT_scale=x_scales[:, cols],
+                lhsT=x_mx[t][0].bitcast(E4M3),
+                lhsT_scale=x_mx[t][1],
                 rhs=g_codes[:].bitcast(E5M2),
                 rhs_scale=g_scales[:],
                 start=True,
@@ -127,13 +142,17 @@ def tile_attend_gsophia_pl_kernel(tc, xT, G, mT, hT, offs, out_0, out_1, out_2, 
             nc.scalar.activation(dw[:], acc[:], ACT.Copy, scale=1.0 / DECAY)
             return dw
 
+        whole = slice(0, SLOTS)
+        halves = [(slice(a * half, (a + 1) * half), offsets[:, a * half // 16 : (a + 1) * half // 16]) for a in range(2)]
+
         def gather_m(t, dw):
             total = tile("total%d" % t, [P, SLOTS], F32)
-            nc.vector.tensor_tensor(total[:], m_tab[t][:].indirect(offsets[:]), dw[:], ALU.add)
+            for cols, entries in ((whole, offsets[:]),) if t == 0 else halves:
+                nc.vector.tensor_tensor(total[:, cols], m_tab[t][:].indirect(entries), dw[:, cols], ALU.add)
             return total
 
         def gather_h(t):
-            h = tile("h%d" % t, [P, SLOTS], F32)
+            h = tile("h%d" % t, [P, SLOTS], F32, tag=("x_grouped12", "x_grouped3", None, None)[t])
             nc.vector.tensor_copy(h[:], h_tab[t][:].indirect(offsets[:]))
             root = tile("root%d" % t, [P, SLOTS], F32, tag="root")
             nc.scalar.activation(root[:], h[:], ACT.Abs_reciprocal_sqrt, scale=1.0 / DECAY, bias=EPS / DECAY)
@@ -143,43 +162,42 @@ def tile_attend_gsophia_pl_kernel(tc, xT, G, mT, hT, offs, out_0, out_1, out_2, 
             nc.scalar.activation(sign[:], h[:], ACT.Sign, bias=EPS)
             return inv, sign
 
-        def late_window(name, tag):
-            win = tile(name, [P, COLS], F32, tag=tag)
-            nc.gpsimd.memset(win[:], 0.0)
-            return win
-
-        def scatter_nm(t, total):
-            nc.vector.tensor_tensor(nm_win[t][:].indirect(offsets[:]), total[:], decay[:], ALU.mult)
-            nc.sync.dma_start(out=nm_rows[t], in_=nm_win[t][:])
+        def scatter_nm(t, total, decay):
+            nc.vector.tensor_tensor(nm_win[t % 2][:].indirect(offsets[:]), total[:], decay[:], ALU.mult)
+            nc.sync.dma_start(out=nm_rows[t], in_=nm_win[t % 2][:])
 
         n_chunks = COLS // CHUNK
         pairs = []
 
         def ratio(t, total, inv):
-            q = tile("ratio%d" % t, [P, SLOTS], F32, tag="h_tab%d" % ((t + 1) % LANES))
-            nc.vector.tensor_tensor(q[:], total[:], inv[:], ALU.mult)
-            cut = tile("cut%d" % t, [P, SLOTS], F32, tag="m_tab0" if t == LANES - 1 else None)
-            nc.vector.tensor_scalar(cut[:], q[:], 1.0, -1.0, ALU.min, ALU.max)
+            q = tile("ratio%d" % t, [P, SLOTS], F32)
+            for cols, entries in halves:
+                nc.vector.tensor_tensor(q[:, cols], total[:, cols], inv[:, cols], ALU.mult)
+            return q
+
+        def clip(t, q):
+            cut = tile("cut%d" % t, [P, SLOTS], F32)
+            for cols, entries in halves:
+                nc.vector.tensor_scalar(cut[:, cols], q[:, cols], 1.0, -1.0, ALU.min, ALU.max)
             return cut
 
         def scatter_up(t, cut, sign):
-            nc.vector.tensor_tensor(up_win[t][:].indirect(offsets[:]), cut[:], sign[:], ALU.mult)
-            nc.sync.dma_start(out=up_rows[t], in_=up_win[t][:])
+            nc.vector.tensor_tensor(up_win[t % 2][:].indirect(offsets[:]), cut[:], sign[:], ALU.mult)
+            (nc.scalar if t < 2 else nc.sync).dma_start(out=up_rows[t], in_=up_win[t % 2][:])
 
         def round_up(t, c):
-            nc.scalar.copy(pairs[c][:, t // 2, :, t % 2], up_win[t][:, c * CHUNK : (c + 1) * CHUNK])
+            nc.scalar.copy(pairs[c][:, t // 2, :, t % 2], up_win[t % 2][:, c * CHUNK : (c + 1) * CHUNK])
 
-        y_scales = tile("y_scales", [P, COLS], U8)
 
         def weave(c):
-            woven = tile("woven%d" % c, [P, CHUNK * LANES], BF16, tag=("m_tab1", "m_tab2", "m_tab3", "h_tab3")[c])
+            woven = tile("woven%d" % c, [P, CHUNK * LANES], BF16)
             nc.scalar.copy(
                 woven[:].bitcast(U32).rearrange("p (c u) -> p c u", u=2),
                 pairs[c][:].rearrange("p u c e -> p u (c e)").bitcast(U32).rearrange("p u c -> p c u"),
             )
             return woven
 
-        def quantise_y(c, woven):
+        def quantise_y(c, woven, y_scales):
             cols = slice(c * CHUNK, (c + 1) * CHUNK)
             codes = tile("y_codes%d" % c, [P, CHUNK], U32)
             nc.vector.quantize_mx(out=codes[:].bitcast(E4M3), scales=y_scales[:, cols], in_=woven[:])
@@ -187,49 +205,44 @@ def tile_attend_gsophia_pl_kernel(tc, xT, G, mT, hT, offs, out_0, out_1, out_2, 
                 out=out_2[0, :, cols, :].rearrange("p c l -> p (c l)").bitcast(I32), in_=codes[:].bitcast(I32)
             )
 
-        total0 = gather_m(0, gradient(0))
-        scatter_nm(0, total0)
-        for t in range(1, LANES):
-            quantise_x(t, turn_x(t))
-        inv0, sign0 = gather_h(0)
+        up_win[1] = window("up_win1", "g_grouped1")
+        dw0 = gradient(0)
+        nm_win[1] = window("nm_win1", "x_scales0")
+        total0 = gather_m(0, dw0)
+        scatter_nm(0, total0, decay)
+        x_bf_rest = tile("x_bf_rest", [P, (LANES - 1) * R], BF16, tag="x_codes0")
+        nc.scalar.copy(x_bf_rest[:], x_rest[:].rearrange("p t r -> p (t r)"))
+        x_scales_rest = tile("x_scales_rest", [P, (LANES - 1) * P], U8)
+        x_mx.extend(quantise_x("12", x_bf_rest, [0, 1], x_scales_rest[:, 0 : 2 * P]))
+        x_mx.extend(quantise_x("3", x_bf_rest, [2], x_scales_rest[:, 2 * P : 3 * P]))
         dws = {t: gradient(t) for t in range(1, LANES)}
-        for c, tag in enumerate(("g_raw", "x_rest", "g_grouped", "pairs")):
+        for c, tag in enumerate(("g_raw0", "g_raw1", "x_rest", "pairs")):
             pairs.append(tile("pairs%d" % c, [P, 2, CHUNK, 2], BF16, tag=tag))
-        inv1, sign1 = gather_h(1)
-        cut0 = ratio(0, total0, inv0)
-        up_win[2] = late_window("up_win2", "h_tab1")
-        scatter_up(0, cut0, sign0)
-        for c in range(n_chunks):
-            round_up(0, c)
-        total1 = gather_m(1, dws[1])
-        scatter_nm(1, total1)
-        inv2, sign2 = gather_h(2)
-        cut1 = ratio(1, total1, inv1)
-        up_win[3] = late_window("up_win3", "h_tab2")
-        scatter_up(1, cut1, sign1)
-        for c in range(n_chunks):
-            round_up(1, c)
-        total2 = gather_m(2, dws[2])
-        inv3, sign3 = gather_h(3)
-        cut2 = ratio(2, total2, inv2)
-        scatter_up(2, cut2, sign2)
-        for c in range(n_chunks):
-            round_up(2, c)
-        total3 = gather_m(3, dws[3])
-        cut3 = ratio(3, total3, inv3)
-        nm_win[2] = late_window("nm_win2", "h_tab0")
-        scatter_up(3, cut3, sign3)
-        nm_win[3] = late_window("nm_win3", "m_tab0")
+        totals = {0: total0}
+        hs = {0: gather_h(0)}
+        for t in range(LANES):
+            if t + 1 < LANES:
+                hs[t + 1] = gather_h(t + 1)
+            if t:
+                totals[t] = gather_m(t, dws[t])
+            cut = clip(t, ratio(t, totals[t], hs[t][0]))
+            if t == LANES - 1:
+                decay_late = tile("decay_late", [P, SLOTS], F32, tag="ratio3")
+                nc.scalar.copy(decay_late[:], decay[:])
+            scatter_up(t, cut, hs[t][1])
+            if t < LANES - 1:
+                for c in range(n_chunks):
+                    round_up(t, c)
         wovens = []
         for c in range(n_chunks):
             round_up(3, c)
             wovens.append(weave(c))
-        scatter_nm(2, total2)
-        for c in range(2):
-            quantise_y(c, wovens[c])
-        scatter_nm(3, total3)
-        for c in range(2, n_chunks):
-            quantise_y(c, wovens[c])
+        scatter_nm(1, totals[1], decay_late)
+        scatter_nm(2, totals[2], decay_late)
+        y_scales = tile("y_scales", [P, COLS], U8)
+        for c in range(n_chunks):
+            quantise_y(c, wovens[c], y_scales)
+        scatter_nm(3, totals[3], decay_late)
         for q in range(4):
             nc.sync.dma_start(
                 out=out_3[0, 4 * q : 4 * q + 4, :].bitcast(I32), in_=y_scales[32 * q : 32 * q + 4, :].bitcast(I32)

@@ -21,7 +21,7 @@ R = 512
 SLOTS = 512
 COLS = 2048
 CHUNK = 512
-G_SPLIT = 160
+G_PIECES = ((0, 256), (256, 384), (384, 512))
 DECAY = 0.9
 EPS = 0.001
 
@@ -47,9 +47,10 @@ def tile_attend_gsophia_pl_kernel(tc, xT, G, mT, hT, offs, out_0, out_1, out_2, 
         nc.sync.dma_start(out=x_first[:], in_=x_rows[:, 0, :])
         half = SLOTS // 2
         g_rows = G.rearrange("(p j) w -> p j w", j=LANES)
-        g_raw = [tile("g_raw%d" % a, [P, LANES, half], F32) for a in range(2)]
-        for a in range(2):
-            nc.sync.dma_start(out=g_raw[a][:], in_=g_rows[:, :, a * half : (a + 1) * half])
+        g_raw = []
+        for a, (lo, hi) in enumerate(G_PIECES):
+            g_raw.append(tile("g_raw%d" % a, [P, LANES, hi - lo], F32))
+            nc.sync.dma_start(out=g_raw[a][:], in_=g_rows[:, :, lo:hi])
         offsets = sb.tile([P, SLOTS // 16], U16, name="offsets")
         nc.sync.dma_start(offsets[:], offs)
         m_tab = [tile("m_tab%d" % t, [P, COLS], F32) for t in range(LANES)]
@@ -74,13 +75,13 @@ def tile_attend_gsophia_pl_kernel(tc, xT, G, mT, hT, offs, out_0, out_1, out_2, 
         warm = tile("warm", [P, 1], F32)
         nc.scalar.activation(warm[:], one[:], ACT.Abs_reciprocal_sqrt)
 
-        def window(name, tag=None):
+        def window(name, engine, tag=None):
             win = tile(name, [P, COLS], F32, tag=tag)
-            nc.vector.memset(win[:].bitcast(I32), 0)
+            engine.memset(win[:].bitcast(I32), 0)
             return win
 
-        nm_win[0] = window("nm_win0")
-        up_win[0] = window("up_win0")
+        nm_win[0] = window("nm_win0", nc.vector)
+        up_win[0] = window("up_win0", nc.vector)
         decay = tile("decay", [P, SLOTS], F32)
         nc.vector.tensor_scalar(decay[:], nm_win[0][:, 0:SLOTS], 1.0, DECAY, ALU.mult, ALU.add)
 
@@ -108,24 +109,19 @@ def tile_attend_gsophia_pl_kernel(tc, xT, G, mT, hT, offs, out_0, out_1, out_2, 
 
         g_codes = tile("g_codes", [P, SLOTS], U32)
         g_scales = tile("g_scales", [P, SLOTS], U8)
-        for a in range(2):
-            g_grouped = tile("g_grouped%d" % a, [P, half, LANES], BF16)
-            split = half if a == 0 else G_SPLIT
+        for a, (lo, hi) in enumerate(G_PIECES):
+            g_grouped = tile("g_grouped%d" % a, [P, hi - lo, LANES], BF16)
             nc.vector.tensor_copy(
-                g_grouped[:, 0:split, :].rearrange("p (c i) j -> p c j i", i=4),
-                g_raw[a][:, :, 0:split].rearrange("p j (c i) -> p c j i", i=4),
+                g_grouped[:].rearrange("p (c i) j -> p c j i", i=4),
+                g_raw[a][:].rearrange("p j (c i) -> p c j i", i=4),
             )
-            if split < half:
-                nc.scalar.copy(
-                    g_grouped[:, split:half, :].rearrange("p (c i) j -> p c j i", i=4),
-                    g_raw[a][:, :, split:half].rearrange("p j (c i) -> p c j i", i=4),
-                )
-            cols = slice(a * half, (a + 1) * half)
             nc.vector.quantize_mx(
-                out=g_codes[:, cols].bitcast(E5M2),
-                scales=g_scales[:, cols],
+                out=g_codes[:, lo:hi].bitcast(E5M2),
+                scales=g_scales[:, lo:hi],
                 in_=g_grouped[:].rearrange("p w j -> p (w j)"),
             )
+
+        halves = [(slice(a * half, (a + 1) * half), offsets[:, a * half // 16 : (a + 1) * half // 16]) for a in range(2)]
 
         def gradient(t):
             acc = ps.tile([P, SLOTS], F32, name="acc%d" % t)
@@ -138,23 +134,21 @@ def tile_attend_gsophia_pl_kernel(tc, xT, G, mT, hT, offs, out_0, out_1, out_2, 
                 start=True,
                 stop=True,
             )
-            dw = tile("dw%d" % t, [P, SLOTS], F32)
-            nc.scalar.activation(dw[:], acc[:], ACT.Copy, scale=1.0 / DECAY)
+            dw = tile("dw%d" % t, [P, SLOTS], F32, tag=(None, "root0", "x_grouped12", "inv0")[t])
+            for cols, entries in halves:
+                nc.scalar.activation(dw[:, cols], acc[:, cols], ACT.Copy, scale=1.0 / DECAY)
             return dw
-
-        whole = slice(0, SLOTS)
-        halves = [(slice(a * half, (a + 1) * half), offsets[:, a * half // 16 : (a + 1) * half // 16]) for a in range(2)]
 
         def gather_m(t, dw):
             total = tile("total%d" % t, [P, SLOTS], F32)
-            for cols, entries in ((whole, offsets[:]),) if t == 0 else halves:
+            for cols, entries in halves:
                 nc.vector.tensor_tensor(total[:, cols], m_tab[t][:].indirect(entries), dw[:, cols], ALU.add)
             return total
 
         def gather_h(t):
             h = tile("h%d" % t, [P, SLOTS], F32, tag=("x_grouped12", "x_grouped3", None, None)[t])
             nc.vector.tensor_copy(h[:], h_tab[t][:].indirect(offsets[:]))
-            root = tile("root%d" % t, [P, SLOTS], F32, tag="root")
+            root = tile("root%d" % t, [P, SLOTS], F32, tag="root" if t else None)
             nc.scalar.activation(root[:], h[:], ACT.Abs_reciprocal_sqrt, scale=1.0 / DECAY, bias=EPS / DECAY)
             inv = tile("inv%d" % t, [P, SLOTS], F32)
             nc.scalar.activation(inv[:], root[:], ACT.Square)
@@ -163,8 +157,8 @@ def tile_attend_gsophia_pl_kernel(tc, xT, G, mT, hT, offs, out_0, out_1, out_2, 
             return inv, sign
 
         def scatter_nm(t, total, decay):
-            nc.vector.tensor_tensor(nm_win[t % 2][:].indirect(offsets[:]), total[:], decay[:], ALU.mult)
-            nc.sync.dma_start(out=nm_rows[t], in_=nm_win[t % 2][:])
+            nc.vector.tensor_tensor(nm_win[t % 3][:].indirect(offsets[:]), total[:], decay[:], ALU.mult)
+            nc.sync.dma_start(out=nm_rows[t], in_=nm_win[t % 3][:])
 
         n_chunks = COLS // CHUNK
         pairs = []
@@ -185,12 +179,18 @@ def tile_attend_gsophia_pl_kernel(tc, xT, G, mT, hT, offs, out_0, out_1, out_2, 
             nc.vector.tensor_tensor(up_win[t % 2][:].indirect(offsets[:]), cut[:], sign[:], ALU.mult)
             (nc.scalar if t < 2 else nc.sync).dma_start(out=up_rows[t], in_=up_win[t % 2][:])
 
-        def round_up(t, c):
-            nc.scalar.copy(pairs[c][:, t // 2, :, t % 2], up_win[t % 2][:, c * CHUNK : (c + 1) * CHUNK])
+        rounded = {}
 
+        def round_up(t, c):
+            u = t // 2
+            if t % 2 == 0:
+                rounded[u, c] = tile("rounded%d_%d" % (u, c), [P, 2, CHUNK], BF16)
+            nc.scalar.copy(rounded[u, c][:, t % 2, :], up_win[t % 2][:, c * CHUNK : (c + 1) * CHUNK])
+            if t % 2 == 1:
+                nc.scalar.copy(pairs[c][:, u, :, :], rounded[u, c][:].rearrange("p e c -> p c e"))
 
         def weave(c):
-            woven = tile("woven%d" % c, [P, CHUNK * LANES], BF16)
+            woven = tile("woven%d" % c, [P, CHUNK * LANES], BF16, tag="h_tab%d" % c)
             nc.scalar.copy(
                 woven[:].bitcast(U32).rearrange("p (c u) -> p c u", u=2),
                 pairs[c][:].rearrange("p u c e -> p u (c e)").bitcast(U32).rearrange("p u c -> p c u"),
@@ -205,19 +205,18 @@ def tile_attend_gsophia_pl_kernel(tc, xT, G, mT, hT, offs, out_0, out_1, out_2, 
                 out=out_2[0, :, cols, :].rearrange("p c l -> p (c l)").bitcast(I32), in_=codes[:].bitcast(I32)
             )
 
-        up_win[1] = window("up_win1", "g_grouped1")
+        up_win[1] = window("up_win1", nc.vector, "g_grouped2")
         dw0 = gradient(0)
-        nm_win[1] = window("nm_win1", "x_scales0")
         total0 = gather_m(0, dw0)
+        nm_win[1] = window("nm_win1", nc.gpsimd, "m_tab0")
         scatter_nm(0, total0, decay)
         x_bf_rest = tile("x_bf_rest", [P, (LANES - 1) * R], BF16, tag="x_codes0")
         nc.scalar.copy(x_bf_rest[:], x_rest[:].rearrange("p t r -> p (t r)"))
         x_scales_rest = tile("x_scales_rest", [P, (LANES - 1) * P], U8)
         x_mx.extend(quantise_x("12", x_bf_rest, [0, 1], x_scales_rest[:, 0 : 2 * P]))
         x_mx.extend(quantise_x("3", x_bf_rest, [2], x_scales_rest[:, 2 * P : 3 * P]))
-        dws = {t: gradient(t) for t in range(1, LANES)}
-        for c, tag in enumerate(("g_raw0", "g_raw1", "x_rest", "pairs")):
-            pairs.append(tile("pairs%d" % c, [P, 2, CHUNK, 2], BF16, tag=tag))
+        for c in range(n_chunks):
+            pairs.append(tile("pairs%d" % c, [P, 2, CHUNK, 2], BF16))
         totals = {0: total0}
         hs = {0: gather_h(0)}
         for t in range(LANES):
@@ -225,7 +224,12 @@ def tile_attend_gsophia_pl_kernel(tc, xT, G, mT, hT, offs, out_0, out_1, out_2, 
                 hs[t + 1] = gather_h(t + 1)
             if t:
                 totals[t] = gather_m(t, dws[t])
-            cut = clip(t, ratio(t, totals[t], hs[t][0]))
+            q = ratio(t, totals[t], hs[t][0])
+            if t == 0:
+                dws = {s: gradient(s) for s in range(1, LANES)}
+            cut = clip(t, q)
+            if t == 0:
+                nm_win[2] = window("nm_win2", nc.gpsimd, "ratio0")
             if t == LANES - 1:
                 decay_late = tile("decay_late", [P, SLOTS], F32, tag="ratio3")
                 nc.scalar.copy(decay_late[:], decay[:])
@@ -239,11 +243,11 @@ def tile_attend_gsophia_pl_kernel(tc, xT, G, mT, hT, offs, out_0, out_1, out_2, 
             wovens.append(weave(c))
         scatter_nm(1, totals[1], decay_late)
         scatter_nm(2, totals[2], decay_late)
+        scatter_nm(3, totals[3], decay_late)
         y_scales = tile("y_scales", [P, COLS], U8)
         for c in range(n_chunks):
             quantise_y(c, wovens[c], y_scales)
-        scatter_nm(3, totals[3], decay_late)
         for q in range(4):
-            nc.sync.dma_start(
+            nc.scalar.dma_start(
                 out=out_3[0, 4 * q : 4 * q + 4, :].bitcast(I32), in_=y_scales[32 * q : 32 * q + 4, :].bitcast(I32)
             )

@@ -20,8 +20,14 @@ D = 512
 R = 512
 SLOTS = 512
 COLS = 2048
+HALF = SLOTS // 2
 CHUNK = 512
+CHUNKS = COLS // CHUNK
+LIST_ROWS = 16
+RUN = 4
 G_PIECES = ((0, 256), (256, 384), (384, 512))
+UP_WINDOWS = 2
+NM_WINDOWS = 3
 DECAY = 0.9
 EPS = 0.001
 
@@ -38,6 +44,7 @@ def tile_attend_gsophia_pl_kernel(tc, xT, G, mT, hT, offs, out_0, out_1, out_2, 
             return sb.tile(shape, dtype, name=name, tag=tag or name, align_bytes=64)
 
         x_rows = xT.rearrange("(m t) r -> m t r", t=LANES)
+        g_rows = G.rearrange("(p j) w -> p j w", j=LANES)
         m_rows = mT.rearrange("(p t) c -> t p c", t=LANES)
         h_rows = hT.rearrange("(p t) c -> t p c", t=LANES)
         up_rows = out_0.rearrange("(p t) c -> t p c", t=LANES)
@@ -45,13 +52,11 @@ def tile_attend_gsophia_pl_kernel(tc, xT, G, mT, hT, offs, out_0, out_1, out_2, 
 
         x_first = tile("x_first", [P, R], F32)
         nc.sync.dma_start(out=x_first[:], in_=x_rows[:, 0, :])
-        half = SLOTS // 2
-        g_rows = G.rearrange("(p j) w -> p j w", j=LANES)
         g_raw = []
         for a, (lo, hi) in enumerate(G_PIECES):
             g_raw.append(tile("g_raw%d" % a, [P, LANES, hi - lo], F32))
             nc.sync.dma_start(out=g_raw[a][:], in_=g_rows[:, :, lo:hi])
-        offsets = sb.tile([P, SLOTS // 16], U16, name="offsets")
+        offsets = sb.tile([P, SLOTS // LIST_ROWS], U16, name="offsets")
         nc.sync.dma_start(offsets[:], offs)
         m_tab = [tile("m_tab%d" % t, [P, COLS], F32) for t in range(LANES)]
         h_tab = [tile("h_tab%d" % t, [P, COLS], F32) for t in range(LANES)]
@@ -68,52 +73,45 @@ def tile_attend_gsophia_pl_kernel(tc, xT, G, mT, hT, offs, out_0, out_1, out_2, 
         ident = tile("ident", [P, P], F32)
         make_identity(nc, ident[:])
 
-        up_win = {}
-        nm_win = {}
-        one = tile("one", [P, 1], F32)
-        nc.vector.memset(one[:], 1.0)
-        warm = tile("warm", [P, 1], F32)
-        nc.scalar.activation(warm[:], one[:], ACT.Abs_reciprocal_sqrt)
-
         def window(name, engine, tag=None):
             win = tile(name, [P, COLS], F32, tag=tag)
             engine.memset(win[:].bitcast(I32), 0)
             return win
 
-        nm_win[0] = window("nm_win0", nc.vector)
-        up_win[0] = window("up_win0", nc.vector)
+        nm_win = [window("nm_win0", nc.vector)]
+        up_win = [window("up_win0", nc.vector)]
         decay = tile("decay", [P, SLOTS], F32)
         nc.vector.tensor_scalar(decay[:], nm_win[0][:, 0:SLOTS], 1.0, DECAY, ALU.mult, ALU.add)
 
-        def quantise_x(name, x_bf, planes, scales):
+        def quantise_x(name, x_bf, parts, scales):
             words = x_bf[:].bitcast(F32)
-            turned = ps.tile([P, len(planes), 2, P], F32, name="turned" + name)
-            for i, t in enumerate(planes):
+            turned = ps.tile([P, len(parts), 2, P], F32, name="turned" + name)
+            for i, part in enumerate(parts):
                 for u in range(2):
                     nc.tensor.transpose(
-                        turned[:, i, u, :], words[:, t * (R // 2) + u : (t + 1) * (R // 2) : 2], ident[:]
+                        turned[:, i, u, :], words[:, part * (R // 2) + u : (part + 1) * (R // 2) : 2], ident[:]
                     )
-            grouped = tile("x_grouped" + name, [P, len(planes) * P * LANES], BF16)
+            grouped = tile("x_grouped" + name, [P, len(parts) * P * LANES], BF16)
             nc.scalar.copy(
-                grouped[:].bitcast(F32).rearrange("p (t m u) -> p t m u", u=2, m=P),
-                turned[:].rearrange("p t u m -> p t m u"),
+                grouped[:].bitcast(F32).rearrange("p (i m u) -> p i m u", u=2, m=P),
+                turned[:].rearrange("p i u m -> p i m u"),
             )
-            codes = tile("x_codes" + name, [P, len(planes) * P], U32)
+            codes = tile("x_codes" + name, [P, len(parts) * P], U32)
             nc.vector.quantize_mx(out=codes[:].bitcast(E4M3), scales=scales, in_=grouped[:])
-            return [(codes[:, i * P : (i + 1) * P], scales[:, i * P : (i + 1) * P]) for i in range(len(planes))]
+            return [(codes[:, i * P : (i + 1) * P], scales[:, i * P : (i + 1) * P]) for i in range(len(parts))]
 
-        x_bf = tile("x_bf", [P, R], BF16)
-        nc.scalar.copy(x_bf[:], x_first[:])
-        x_scales0 = tile("x_scales0", [P, P], U8)
-        x_mx = quantise_x("0", x_bf, [0], x_scales0[:])
+        x_bf_first = tile("x_bf_first", [P, R], BF16)
+        nc.scalar.copy(x_bf_first[:], x_first[:])
+        x_scales_first = tile("x_scales_first", [P, P], U8)
+        x_mx = quantise_x("0", x_bf_first, [0], x_scales_first[:])
 
         g_codes = tile("g_codes", [P, SLOTS], U32)
         g_scales = tile("g_scales", [P, SLOTS], U8)
         for a, (lo, hi) in enumerate(G_PIECES):
             g_grouped = tile("g_grouped%d" % a, [P, hi - lo, LANES], BF16)
             nc.vector.tensor_copy(
-                g_grouped[:].rearrange("p (c i) j -> p c j i", i=4),
-                g_raw[a][:].rearrange("p j (c i) -> p c j i", i=4),
+                g_grouped[:].rearrange("p (c i) j -> p c j i", i=RUN),
+                g_raw[a][:].rearrange("p j (c i) -> p c j i", i=RUN),
             )
             nc.vector.quantize_mx(
                 out=g_codes[:, lo:hi].bitcast(E5M2),
@@ -121,7 +119,7 @@ def tile_attend_gsophia_pl_kernel(tc, xT, G, mT, hT, offs, out_0, out_1, out_2, 
                 in_=g_grouped[:].rearrange("p w j -> p (w j)"),
             )
 
-        halves = [(slice(a * half, (a + 1) * half), offsets[:, a * half // 16 : (a + 1) * half // 16]) for a in range(2)]
+        halves = [slice(a * HALF, (a + 1) * HALF) for a in range(2)]
 
         def gradient(t):
             acc = ps.tile([P, SLOTS], F32, name="acc%d" % t)
@@ -134,60 +132,59 @@ def tile_attend_gsophia_pl_kernel(tc, xT, G, mT, hT, offs, out_0, out_1, out_2, 
                 start=True,
                 stop=True,
             )
-            dw = tile("dw%d" % t, [P, SLOTS], F32, tag=(None, "root0", "x_grouped12", "inv0")[t])
-            for cols, entries in halves:
+            dw = tile("dw%d" % t, [P, SLOTS], F32, tag=(None, "root01", "x_grouped12", "inv0")[t])
+            for cols in halves:
                 nc.scalar.activation(dw[:, cols], acc[:, cols], ACT.Copy, scale=1.0 / DECAY)
             return dw
 
         def gather_m(t, dw):
             total = tile("total%d" % t, [P, SLOTS], F32)
-            for cols, entries in halves:
+            for cols in halves:
+                entries = offsets[:, cols.start // LIST_ROWS : cols.stop // LIST_ROWS]
                 nc.vector.tensor_tensor(total[:, cols], m_tab[t][:].indirect(entries), dw[:, cols], ALU.add)
             return total
 
         def gather_h(t):
             h = tile("h%d" % t, [P, SLOTS], F32, tag=("x_grouped12", "x_grouped3", None, None)[t])
             nc.vector.tensor_copy(h[:], h_tab[t][:].indirect(offsets[:]))
-            root = tile("root%d" % t, [P, SLOTS], F32, tag="root" if t else None)
-            nc.scalar.activation(root[:], h[:], ACT.Abs_reciprocal_sqrt, scale=1.0 / DECAY, bias=EPS / DECAY)
+            root = tile("root%d" % t, [P, SLOTS], F32, tag="root01" if t < 2 else "root23")
             inv = tile("inv%d" % t, [P, SLOTS], F32)
-            nc.scalar.activation(inv[:], root[:], ACT.Square)
+            for cols in halves:
+                nc.scalar.activation(
+                    root[:, cols], h[:, cols], ACT.Abs_reciprocal_sqrt, scale=1.0 / DECAY, bias=EPS / DECAY
+                )
+            for cols in halves:
+                nc.scalar.activation(inv[:, cols], root[:, cols], ACT.Square)
             sign = tile("sign%d" % t, [P, SLOTS], F32)
             nc.scalar.activation(sign[:], h[:], ACT.Sign, bias=EPS)
             return inv, sign
 
-        def scatter_nm(t, total, decay):
-            nc.vector.tensor_tensor(nm_win[t % 3][:].indirect(offsets[:]), total[:], decay[:], ALU.mult)
-            nc.sync.dma_start(out=nm_rows[t], in_=nm_win[t % 3][:])
-
-        n_chunks = COLS // CHUNK
-        pairs = []
+        def scatter_nm(t, total, factor):
+            win = nm_win[t % NM_WINDOWS]
+            nc.vector.tensor_tensor(win[:].indirect(offsets[:]), total[:], factor[:], ALU.mult)
+            nc.sync.dma_start(out=nm_rows[t], in_=win[:])
 
         def ratio(t, total, inv):
-            q = tile("ratio%d" % t, [P, SLOTS], F32)
-            for cols, entries in halves:
-                nc.vector.tensor_tensor(q[:, cols], total[:, cols], inv[:, cols], ALU.mult)
-            return q
+            quotient = tile("ratio%d" % t, [P, SLOTS], F32)
+            for cols in halves:
+                nc.vector.tensor_tensor(quotient[:, cols], total[:, cols], inv[:, cols], ALU.mult)
+            return quotient
 
-        def clip(t, q):
+        def clip(t, quotient):
             cut = tile("cut%d" % t, [P, SLOTS], F32)
-            for cols, entries in halves:
-                nc.vector.tensor_scalar(cut[:, cols], q[:, cols], 1.0, -1.0, ALU.min, ALU.max)
+            for cols in halves:
+                nc.vector.tensor_scalar(cut[:, cols], quotient[:, cols], 1.0, -1.0, ALU.min, ALU.max)
             return cut
 
         def scatter_up(t, cut, sign):
-            nc.vector.tensor_tensor(up_win[t % 2][:].indirect(offsets[:]), cut[:], sign[:], ALU.mult)
-            (nc.scalar if t < 2 else nc.sync).dma_start(out=up_rows[t], in_=up_win[t % 2][:])
-
-        rounded = {}
+            win = up_win[t % UP_WINDOWS]
+            nc.vector.tensor_tensor(win[:].indirect(offsets[:]), cut[:], sign[:], ALU.mult)
+            queue = nc.scalar if t + UP_WINDOWS < LANES else nc.sync
+            queue.dma_start(out=up_rows[t], in_=win[:])
 
         def round_up(t, c):
-            u = t // 2
-            if t % 2 == 0:
-                rounded[u, c] = tile("rounded%d_%d" % (u, c), [P, 2, CHUNK], BF16)
-            nc.scalar.copy(rounded[u, c][:, t % 2, :], up_win[t % 2][:, c * CHUNK : (c + 1) * CHUNK])
-            if t % 2 == 1:
-                nc.scalar.copy(pairs[c][:, u, :, :], rounded[u, c][:].rearrange("p e c -> p c e"))
+            win = up_win[t % UP_WINDOWS]
+            nc.scalar.copy(pairs[c][:, t // 2, :, t % 2], win[:, c * CHUNK : (c + 1) * CHUNK])
 
         def weave(c):
             woven = tile("woven%d" % c, [P, CHUNK * LANES], BF16, tag="h_tab%d" % c)
@@ -205,49 +202,50 @@ def tile_attend_gsophia_pl_kernel(tc, xT, G, mT, hT, offs, out_0, out_1, out_2, 
                 out=out_2[0, :, cols, :].rearrange("p c l -> p (c l)").bitcast(I32), in_=codes[:].bitcast(I32)
             )
 
-        up_win[1] = window("up_win1", nc.vector, "g_grouped2")
-        dw0 = gradient(0)
-        total0 = gather_m(0, dw0)
-        nm_win[1] = window("nm_win1", nc.gpsimd, "m_tab0")
-        scatter_nm(0, total0, decay)
+        up_win.append(window("up_win1", nc.vector, "x_grouped0"))
+        totals = [gather_m(0, gradient(0))]
+        nm_win.append(window("nm_win1", nc.gpsimd, "m_tab0"))
+        scatter_nm(0, totals[0], decay)
+
         x_bf_rest = tile("x_bf_rest", [P, (LANES - 1) * R], BF16, tag="x_codes0")
         nc.scalar.copy(x_bf_rest[:], x_rest[:].rearrange("p t r -> p (t r)"))
         x_scales_rest = tile("x_scales_rest", [P, (LANES - 1) * P], U8)
         x_mx.extend(quantise_x("12", x_bf_rest, [0, 1], x_scales_rest[:, 0 : 2 * P]))
         x_mx.extend(quantise_x("3", x_bf_rest, [2], x_scales_rest[:, 2 * P : 3 * P]))
-        for c in range(n_chunks):
-            pairs.append(tile("pairs%d" % c, [P, 2, CHUNK, 2], BF16))
-        totals = {0: total0}
-        hs = {0: gather_h(0)}
+
+        pairs = [tile("pairs%d" % c, [P, 2, CHUNK, 2], BF16) for c in range(CHUNKS)]
+        scaling = [gather_h(0)]
+        last = LANES - 1
         for t in range(LANES):
-            if t + 1 < LANES:
-                hs[t + 1] = gather_h(t + 1)
-            if t:
-                totals[t] = gather_m(t, dws[t])
-            q = ratio(t, totals[t], hs[t][0])
+            if t < last:
+                scaling.append(gather_h(t + 1))
+            if t > 0:
+                totals.append(gather_m(t, dws[t]))
+            inv, sign = scaling[t]
+            quotient = ratio(t, totals[t], inv)
             if t == 0:
                 dws = {s: gradient(s) for s in range(1, LANES)}
-            cut = clip(t, q)
+            cut = clip(t, quotient)
             if t == 0:
-                nm_win[2] = window("nm_win2", nc.gpsimd, "ratio0")
-            if t == LANES - 1:
-                decay_late = tile("decay_late", [P, SLOTS], F32, tag="ratio3")
+                nm_win.append(window("nm_win2", nc.gpsimd, "ratio0"))
+            if t == last:
+                decay_late = tile("decay_late", [P, SLOTS], F32, tag="ratio%d" % last)
                 nc.scalar.copy(decay_late[:], decay[:])
-            scatter_up(t, cut, hs[t][1])
-            if t < LANES - 1:
-                for c in range(n_chunks):
+            scatter_up(t, cut, sign)
+            if t < last:
+                for c in range(CHUNKS):
                     round_up(t, c)
+
         wovens = []
-        for c in range(n_chunks):
-            round_up(3, c)
+        for c in range(CHUNKS):
+            round_up(last, c)
             wovens.append(weave(c))
-        scatter_nm(1, totals[1], decay_late)
-        scatter_nm(2, totals[2], decay_late)
-        scatter_nm(3, totals[3], decay_late)
+        for t in range(1, LANES):
+            scatter_nm(t, totals[t], decay_late)
         y_scales = tile("y_scales", [P, COLS], U8)
-        for c in range(n_chunks):
+        for c in range(CHUNKS):
             quantise_y(c, wovens[c], y_scales)
-        for q in range(4):
+        for q in range(P // 32):
             nc.scalar.dma_start(
                 out=out_3[0, 4 * q : 4 * q + 4, :].bitcast(I32), in_=y_scales[32 * q : 32 * q + 4, :].bitcast(I32)
             )

@@ -25,9 +25,10 @@ CHUNK = 512
 CHUNKS = COLS // CHUNK
 LIST_ROWS = 16
 RUN = 4
-G_PIECES = ((0, 256), (256, 384), (384, 512))
-UP_WINDOWS = 2
-NM_WINDOWS = 3
+G_PIECES = ((0, 256), (256, 512))
+UP_WINDOWS = 3
+NM_WINDOWS = 2
+WORD = (U32, U32, I32, I32)
 DECAY = 0.9
 EPS = 0.001
 
@@ -43,67 +44,76 @@ def tile_attend_gsophia_pl_kernel(tc, xT, G, mT, hT, offs, out_0, out_1, out_2, 
         def tile(name, shape, dtype, tag=None):
             return sb.tile(shape, dtype, name=name, tag=tag or name, align_bytes=64)
 
-        x_rows = xT.rearrange("(m t) r -> m t r", t=LANES)
         g_rows = G.rearrange("(p j) w -> p j w", j=LANES)
         m_rows = mT.rearrange("(p t) c -> t p c", t=LANES)
         h_rows = hT.rearrange("(p t) c -> t p c", t=LANES)
         up_rows = out_0.rearrange("(p t) c -> t p c", t=LANES)
         nm_rows = out_1.rearrange("(p t) c -> t p c", t=LANES)
 
-        x_first = tile("x_first", [P, R], F32)
-        nc.sync.dma_start(out=x_first[:], in_=x_rows[:, 0, :])
+        offsets = sb.tile([P, SLOTS // LIST_ROWS], U16, name="offsets")
+        nc.sync.dma_start(offsets[:], offs)
+        x_raw = tile("x_raw", [P, LANES, R], F32)
+        nc.sync.dma_start(out=x_raw[:], in_=xT.rearrange("(m t) r -> m t r", t=LANES))
+        m_tab = [tile("m_tab%d" % t, [P, COLS], F32) for t in range(LANES)]
+        h_tab = [tile("h_tab%d" % t, [P, COLS], F32) for t in range(LANES)]
+        nc.sync.dma_start(out=h_tab[0][:], in_=h_rows[0])
         g_raw = []
         for a, (lo, hi) in enumerate(G_PIECES):
             g_raw.append(tile("g_raw%d" % a, [P, LANES, hi - lo], F32))
             nc.sync.dma_start(out=g_raw[a][:], in_=g_rows[:, :, lo:hi])
-        offsets = sb.tile([P, SLOTS // LIST_ROWS], U16, name="offsets")
-        nc.sync.dma_start(offsets[:], offs)
-        m_tab = [tile("m_tab%d" % t, [P, COLS], F32) for t in range(LANES)]
-        h_tab = [tile("h_tab%d" % t, [P, COLS], F32) for t in range(LANES)]
         nc.sync.dma_start(out=m_tab[0][:], in_=m_rows[0])
-        x_rest = tile("x_rest", [P, LANES - 1, R], F32)
-        nc.sync.dma_start(out=x_rest[:], in_=x_rows[:, 1:LANES, :])
-        nc.sync.dma_start(out=h_tab[0][:], in_=h_rows[0])
-        nc.sync.dma_start(out=h_tab[1][:], in_=h_rows[1])
         for t in range(1, LANES):
-            if t + 1 < LANES:
-                nc.sync.dma_start(out=h_tab[t + 1][:], in_=h_rows[t + 1])
+            nc.sync.dma_start(out=h_tab[t][:], in_=h_rows[t])
             nc.sync.dma_start(out=m_tab[t][:], in_=m_rows[t])
 
         ident = tile("ident", [P, P], F32)
         make_identity(nc, ident[:])
+
+        halves = [slice(a * HALF, (a + 1) * HALF) for a in range(2)]
+
+        def entries(cols):
+            return offsets[:, cols.start // LIST_ROWS : cols.stop // LIST_ROWS]
 
         def window(name, engine, tag=None):
             win = tile(name, [P, COLS], F32, tag=tag)
             engine.memset(win[:].bitcast(I32), 0)
             return win
 
-        nm_win = [window("nm_win0", nc.vector)]
-        up_win = [window("up_win0", nc.vector)]
-        decay = tile("decay", [P, SLOTS], F32)
-        nc.vector.tensor_scalar(decay[:], nm_win[0][:, 0:SLOTS], 1.0, DECAY, ALU.mult, ALU.add)
+        nm_win = [window("nm_win%d" % a, nc.vector) for a in range(NM_WINDOWS)]
+        up_win = [window("up_win%d" % a, nc.vector) for a in range(UP_WINDOWS)]
 
-        def quantise_x(name, x_bf, parts, scales):
-            words = x_bf[:].bitcast(F32)
-            turned = ps.tile([P, len(parts), 2, P], F32, name="turned" + name)
-            for i, part in enumerate(parts):
-                for u in range(2):
-                    nc.tensor.transpose(
-                        turned[:, i, u, :], words[:, part * (R // 2) + u : (part + 1) * (R // 2) : 2], ident[:]
-                    )
-            grouped = tile("x_grouped" + name, [P, len(parts) * P * LANES], BF16)
-            nc.scalar.copy(
-                grouped[:].bitcast(F32).rearrange("p (i m u) -> p i m u", u=2, m=P),
-                turned[:].rearrange("p i u m -> p i m u"),
+        def quantise_x(t):
+            turned = ps.tile([P, LANES, P], F32, name="turned%d" % t)
+            for j in range(LANES):
+                nc.tensor.transpose(turned[:, j, :], x_raw[:, t, j:R:LANES], ident[:])
+            grouped = tile("x_grouped%d" % t, [P, P, LANES], BF16)
+            nc.scalar.copy(grouped[:], turned[:].rearrange("p j m -> p m j"))
+            codes = tile("x_codes%d" % t, [P, P], U32)
+            scales = tile("x_scales%d" % t, [P, P], U8)
+            nc.vector.quantize_mx(
+                out=codes[:].bitcast(E4M3), scales=scales[:], in_=grouped[:].rearrange("p m j -> p (m j)")
             )
-            codes = tile("x_codes" + name, [P, len(parts) * P], U32)
-            nc.vector.quantize_mx(out=codes[:].bitcast(E4M3), scales=scales, in_=grouped[:])
-            return [(codes[:, i * P : (i + 1) * P], scales[:, i * P : (i + 1) * P]) for i in range(len(parts))]
+            return codes, scales
 
-        x_bf_first = tile("x_bf_first", [P, R], BF16)
-        nc.scalar.copy(x_bf_first[:], x_first[:])
-        x_scales_first = tile("x_scales_first", [P, P], U8)
-        x_mx = quantise_x("0", x_bf_first, [0], x_scales_first[:])
+        def scaling(t, h):
+            root = tile("root%d" % t, [P, SLOTS], F32)
+            inv = tile("inv%d" % t, [P, SLOTS], F32)
+            sign = tile("sign%d" % t, [P, SLOTS], F32)
+            nc.scalar.activation(root[:], h[:], ACT.Abs_reciprocal_sqrt, scale=1.0 / DECAY, bias=EPS / DECAY)
+            nc.scalar.activation(sign[:], h[:], ACT.Sign, bias=EPS)
+            nc.scalar.activation(inv[:], root[:], ACT.Square)
+            return inv, sign
+
+        def gather_h(t):
+            h = tile("h%d" % t, [P, SLOTS], F32)
+            if t == 0:
+                nc.vector.tensor_copy(h[:], h_tab[t][:].indirect(offsets[:]))
+            else:
+                nc.scalar.activation(h[:], h_tab[t][:].indirect(offsets[:]), ACT.Copy)
+            return h
+
+        x_mx = [quantise_x(t) for t in range(LANES)]
+        scalings = [scaling(0, gather_h(0))]
 
         g_codes = tile("g_codes", [P, SLOTS], U32)
         g_scales = tile("g_scales", [P, SLOTS], U8)
@@ -119,78 +129,59 @@ def tile_attend_gsophia_pl_kernel(tc, xT, G, mT, hT, offs, out_0, out_1, out_2, 
                 in_=g_grouped[:].rearrange("p w j -> p (w j)"),
             )
 
-        halves = [slice(a * HALF, (a + 1) * HALF) for a in range(2)]
-
         def gradient(t):
             acc = ps.tile([P, SLOTS], F32, name="acc%d" % t)
             nc.tensor.matmul_mx(
                 out=acc[:],
-                lhsT=x_mx[t][0].bitcast(E4M3),
-                lhsT_scale=x_mx[t][1],
+                lhsT=x_mx[t][0][:].bitcast(E4M3),
+                lhsT_scale=x_mx[t][1][:],
                 rhs=g_codes[:].bitcast(E5M2),
                 rhs_scale=g_scales[:],
                 start=True,
                 stop=True,
             )
-            dw = tile("dw%d" % t, [P, SLOTS], F32, tag=(None, "root01", "x_grouped12", "inv0")[t])
-            for cols in halves:
-                nc.scalar.activation(dw[:, cols], acc[:, cols], ACT.Copy, scale=1.0 / DECAY)
+            dw = tile("dw%d" % t, [P, SLOTS], F32)
+            nc.scalar.activation(dw[:], acc[:], ACT.Copy, scale=1.0 / DECAY)
             return dw
 
-        def gather_m(t, dw):
+        dws = [gradient(t) for t in range(LANES)]
+
+        def gather_m(t):
             total = tile("total%d" % t, [P, SLOTS], F32)
             for cols in halves:
-                entries = offsets[:, cols.start // LIST_ROWS : cols.stop // LIST_ROWS]
-                nc.vector.tensor_tensor(total[:, cols], m_tab[t][:].indirect(entries), dw[:, cols], ALU.add)
+                nc.vector.tensor_tensor(total[:, cols], m_tab[t][:].indirect(entries(cols)), dws[t][:, cols], ALU.add)
             return total
 
-        def gather_h(t):
-            h = tile("h%d" % t, [P, SLOTS], F32, tag=("x_grouped12", "x_grouped3", None, None)[t])
-            nc.vector.tensor_copy(h[:], h_tab[t][:].indirect(offsets[:]))
-            root = tile("root%d" % t, [P, SLOTS], F32, tag="root01" if t < 2 else "root23")
-            inv = tile("inv%d" % t, [P, SLOTS], F32)
-            for cols in halves:
-                nc.scalar.activation(
-                    root[:, cols], h[:, cols], ACT.Abs_reciprocal_sqrt, scale=1.0 / DECAY, bias=EPS / DECAY
-                )
-            for cols in halves:
-                nc.scalar.activation(inv[:, cols], root[:, cols], ACT.Square)
-            sign = tile("sign%d" % t, [P, SLOTS], F32)
-            nc.scalar.activation(sign[:], h[:], ACT.Sign, bias=EPS)
-            return inv, sign
-
-        def scatter_nm(t, total, factor):
+        def scatter_nm(t, total):
             win = nm_win[t % NM_WINDOWS]
-            nc.vector.tensor_tensor(win[:].indirect(offsets[:]), total[:], factor[:], ALU.mult)
-            nc.sync.dma_start(out=nm_rows[t], in_=win[:])
+            for cols in halves:
+                nc.scalar.activation(win[:].indirect(entries(cols)), total[:, cols], ACT.Copy, scale=DECAY)
+            queue = nc.scalar if t + NM_WINDOWS < LANES else nc.sync
+            queue.dma_start(out=nm_rows[t], in_=win[:])
 
-        def ratio(t, total, inv):
+        def step(t, total):
+            inv, sign = scalings[t]
             quotient = tile("ratio%d" % t, [P, SLOTS], F32)
             for cols in halves:
                 nc.vector.tensor_tensor(quotient[:, cols], total[:, cols], inv[:, cols], ALU.mult)
-            return quotient
-
-        def clip(t, quotient):
             cut = tile("cut%d" % t, [P, SLOTS], F32)
             for cols in halves:
                 nc.vector.tensor_scalar(cut[:, cols], quotient[:, cols], 1.0, -1.0, ALU.min, ALU.max)
-            return cut
-
-        def scatter_up(t, cut, sign):
             win = up_win[t % UP_WINDOWS]
             nc.vector.tensor_tensor(win[:].indirect(offsets[:]), cut[:], sign[:], ALU.mult)
-            queue = nc.scalar if t + UP_WINDOWS < LANES else nc.sync
-            queue.dma_start(out=up_rows[t], in_=win[:])
+            nc.sync.dma_start(out=up_rows[t], in_=win[:])
+
+        pairs = [tile("pairs%d" % c, [P, 2, CHUNK, 2], BF16) for c in range(CHUNKS)]
 
         def round_up(t, c):
             win = up_win[t % UP_WINDOWS]
-            nc.scalar.copy(pairs[c][:, t // 2, :, t % 2], win[:, c * CHUNK : (c + 1) * CHUNK])
+            nc.vector.tensor_copy(pairs[c][:, t // 2, :, t % 2], win[:, c * CHUNK : (c + 1) * CHUNK])
 
-        def weave(c):
+        def weave(c, copy):
             woven = tile("woven%d" % c, [P, CHUNK * LANES], BF16, tag="h_tab%d" % c)
-            nc.scalar.copy(
-                woven[:].bitcast(U32).rearrange("p (c u) -> p c u", u=2),
-                pairs[c][:].rearrange("p u c e -> p u (c e)").bitcast(U32).rearrange("p u c -> p c u"),
+            copy(
+                woven[:].bitcast(WORD[c]).rearrange("p (c u) -> p c u", u=2),
+                pairs[c][:].rearrange("p u c e -> p u (c e)").bitcast(WORD[c]).rearrange("p u c -> p c u"),
             )
             return woven
 
@@ -202,48 +193,18 @@ def tile_attend_gsophia_pl_kernel(tc, xT, G, mT, hT, offs, out_0, out_1, out_2, 
                 out=out_2[0, :, cols, :].rearrange("p c l -> p (c l)").bitcast(I32), in_=codes[:].bitcast(I32)
             )
 
-        up_win.append(window("up_win1", nc.vector, "x_grouped0"))
-        totals = [gather_m(0, gradient(0))]
-        nm_win.append(window("nm_win1", nc.gpsimd, "m_tab0"))
-        scatter_nm(0, totals[0], decay)
-
-        x_bf_rest = tile("x_bf_rest", [P, (LANES - 1) * R], BF16, tag="x_codes0")
-        nc.scalar.copy(x_bf_rest[:], x_rest[:].rearrange("p t r -> p (t r)"))
-        x_scales_rest = tile("x_scales_rest", [P, (LANES - 1) * P], U8)
-        x_mx.extend(quantise_x("12", x_bf_rest, [0, 1], x_scales_rest[:, 0 : 2 * P]))
-        x_mx.extend(quantise_x("3", x_bf_rest, [2], x_scales_rest[:, 2 * P : 3 * P]))
-
-        pairs = [tile("pairs%d" % c, [P, 2, CHUNK, 2], BF16) for c in range(CHUNKS)]
-        scaling = [gather_h(0)]
-        last = LANES - 1
         for t in range(LANES):
-            if t < last:
-                scaling.append(gather_h(t + 1))
-            if t > 0:
-                totals.append(gather_m(t, dws[t]))
-            inv, sign = scaling[t]
-            quotient = ratio(t, totals[t], inv)
-            if t == 0:
-                dws = {s: gradient(s) for s in range(1, LANES)}
-            cut = clip(t, quotient)
-            if t == 0:
-                nm_win.append(window("nm_win2", nc.gpsimd, "ratio0"))
-            if t == last:
-                decay_late = tile("decay_late", [P, SLOTS], F32, tag="ratio%d" % last)
-                nc.scalar.copy(decay_late[:], decay[:])
-            scatter_up(t, cut, sign)
-            if t < last:
-                for c in range(CHUNKS):
-                    round_up(t, c)
+            total = gather_m(t)
+            if t + 1 < LANES:
+                scalings.append(scaling(t + 1, gather_h(t + 1)))
+            step(t, total)
+            scatter_nm(t, total)
+            for c in range(CHUNKS):
+                round_up(t, c)
 
-        wovens = []
-        for c in range(CHUNKS):
-            round_up(last, c)
-            wovens.append(weave(c))
-        for t in range(1, LANES):
-            scatter_nm(t, totals[t], decay_late)
+        wovens = [weave(c, nc.scalar.copy if c < 2 else nc.vector.tensor_copy) for c in range(CHUNKS)]
         y_scales = tile("y_scales", [P, COLS], U8)
-        for c in range(CHUNKS):
+        for c in (2, 3, 0, 1):
             quantise_y(c, wovens[c], y_scales)
         for q in range(P // 32):
             nc.scalar.dma_start(

@@ -82,17 +82,22 @@ def tile_attend_gsophia_pl_kernel(tc, xT, G, mT, hT, offs, out_0, out_1, out_2, 
         nm_win = [window("nm_win%d" % a, nc.vector) for a in range(NM_WINDOWS)]
         up_win = [window("up_win%d" % a, nc.vector) for a in range(UP_WINDOWS)]
 
+        x_bf = tile("x_bf", [P, LANES * R], BF16)
+        nc.vector.tensor_copy(x_bf[:], x_raw[:].rearrange("p t r -> p (t r)"))
+        x_words = x_bf[:].bitcast(F32)
+        x_grouped = [tile("x_grouped%d" % t, [P, P * LANES], BF16) for t in range(LANES)]
+        for t in range(LANES):
+            turned = ps.tile([P, 2, P], F32, name="turned%d" % t)
+            for u in range(2):
+                nc.tensor.transpose(turned[:, u, :], x_words[:, t * (R // 2) + u : (t + 1) * (R // 2) : 2], ident[:])
+            nc.scalar.copy(
+                x_grouped[t][:].bitcast(F32).rearrange("p (m u) -> p m u", u=2), turned[:].rearrange("p u m -> p m u")
+            )
+
         def quantise_x(t):
-            turned = ps.tile([P, LANES, P], F32, name="turned%d" % t)
-            for j in range(LANES):
-                nc.tensor.transpose(turned[:, j, :], x_raw[:, t, j:R:LANES], ident[:])
-            grouped = tile("x_grouped%d" % t, [P, P, LANES], BF16)
-            nc.scalar.copy(grouped[:], turned[:].rearrange("p j m -> p m j"))
             codes = tile("x_codes%d" % t, [P, P], U32)
             scales = tile("x_scales%d" % t, [P, P], U8)
-            nc.vector.quantize_mx(
-                out=codes[:].bitcast(E4M3), scales=scales[:], in_=grouped[:].rearrange("p m j -> p (m j)")
-            )
+            nc.vector.quantize_mx(out=codes[:].bitcast(E4M3), scales=scales[:], in_=x_grouped[t][:])
             return codes, scales
 
         def scaling(t, h):
@@ -100,8 +105,8 @@ def tile_attend_gsophia_pl_kernel(tc, xT, G, mT, hT, offs, out_0, out_1, out_2, 
             inv = tile("inv%d" % t, [P, SLOTS], F32)
             sign = tile("sign%d" % t, [P, SLOTS], F32)
             nc.scalar.activation(root[:], h[:], ACT.Abs_reciprocal_sqrt, scale=1.0 / DECAY, bias=EPS / DECAY)
-            nc.scalar.activation(sign[:], h[:], ACT.Sign, bias=EPS)
             nc.scalar.activation(inv[:], root[:], ACT.Square)
+            nc.scalar.activation(sign[:], h[:], ACT.Sign, bias=EPS)
             return inv, sign
 
         def gather_h(t):
@@ -112,7 +117,6 @@ def tile_attend_gsophia_pl_kernel(tc, xT, G, mT, hT, offs, out_0, out_1, out_2, 
                 nc.scalar.activation(h[:], h_tab[t][:].indirect(offsets[:]), ACT.Copy)
             return h
 
-        x_mx = [quantise_x(t) for t in range(LANES)]
         scalings = [scaling(0, gather_h(0))]
 
         g_codes = tile("g_codes", [P, SLOTS], U32)
@@ -123,11 +127,15 @@ def tile_attend_gsophia_pl_kernel(tc, xT, G, mT, hT, offs, out_0, out_1, out_2, 
                 g_grouped[:].rearrange("p (c i) j -> p c j i", i=RUN),
                 g_raw[a][:].rearrange("p j (c i) -> p c j i", i=RUN),
             )
+            if a == 0:
+                x_mx = [quantise_x(0)]
             nc.vector.quantize_mx(
                 out=g_codes[:, lo:hi].bitcast(E5M2),
                 scales=g_scales[:, lo:hi],
                 in_=g_grouped[:].rearrange("p w j -> p (w j)"),
             )
+
+        x_mx.extend(quantise_x(t) for t in range(1, LANES))
 
         def gradient(t):
             acc = ps.tile([P, SLOTS], F32, name="acc%d" % t)

@@ -1,7 +1,6 @@
 from contextlib import ExitStack
 
 import concourse.mybir as mybir
-from concourse.masks import make_identity
 
 F32 = mybir.dt.float32
 BF16 = mybir.dt.bfloat16
@@ -28,7 +27,7 @@ RUN = 4
 G_PIECES = ((0, 256), (256, 512))
 UP_WINDOWS = 3
 NM_WINDOWS = 2
-WORD = (U32, U32, I32, I32)
+WORD = (I32, I32, U32, U32)
 DECAY = 0.9
 EPS = 0.001
 
@@ -56,18 +55,26 @@ def tile_attend_gsophia_pl_kernel(tc, xT, G, mT, hT, offs, out_0, out_1, out_2, 
         nc.sync.dma_start(out=x_raw[:], in_=xT.rearrange("(m t) r -> m t r", t=LANES))
         m_tab = [tile("m_tab%d" % t, [P, COLS], F32) for t in range(LANES)]
         h_tab = [tile("h_tab%d" % t, [P, COLS], F32) for t in range(LANES)]
-        nc.sync.dma_start(out=h_tab[0][:], in_=h_rows[0])
         g_raw = []
         for a, (lo, hi) in enumerate(G_PIECES):
             g_raw.append(tile("g_raw%d" % a, [P, LANES, hi - lo], F32))
             nc.sync.dma_start(out=g_raw[a][:], in_=g_rows[:, :, lo:hi])
-        nc.sync.dma_start(out=m_tab[0][:], in_=m_rows[0])
-        for t in range(1, LANES):
+        for t in range(LANES):
             nc.sync.dma_start(out=h_tab[t][:], in_=h_rows[t])
             nc.sync.dma_start(out=m_tab[t][:], in_=m_rows[t])
 
         ident = tile("ident", [P, P], F32)
-        make_identity(nc, ident[:])
+        zeros = tile("zeros", [P, P], F32, tag="nm_win1")
+        nc.gpsimd.memset(zeros[:], 0.0)
+        nc.gpsimd.affine_select(
+            out=ident[:],
+            in_=zeros[:],
+            compare_op=ALU.not_equal,
+            fill=1.0,
+            base=0,
+            pattern=[[-1, P]],
+            channel_multiplier=1,
+        )
 
         halves = [slice(a * HALF, (a + 1) * HALF) for a in range(2)]
 
@@ -79,8 +86,8 @@ def tile_attend_gsophia_pl_kernel(tc, xT, G, mT, hT, offs, out_0, out_1, out_2, 
             engine.memset(win[:].bitcast(I32), 0)
             return win
 
-        nm_win = [window("nm_win%d" % a, nc.vector) for a in range(NM_WINDOWS)]
-        up_win = [window("up_win%d" % a, nc.vector) for a in range(UP_WINDOWS)]
+        nm_win = [window("nm_win0", nc.vector), window("nm_win1", nc.gpsimd)]
+        up_win = [window("up_win0", nc.vector)]
 
         x_bf = tile("x_bf", [P, LANES * R], BF16)
         nc.vector.tensor_copy(x_bf[:], x_raw[:].rearrange("p t r -> p (t r)"))
@@ -110,14 +117,12 @@ def tile_attend_gsophia_pl_kernel(tc, xT, G, mT, hT, offs, out_0, out_1, out_2, 
             return inv, sign
 
         def gather_h(t):
-            h = tile("h%d" % t, [P, SLOTS], F32)
+            h = tile("h%d" % t, [P, SLOTS], F32, tag="x_grouped3" if t == 0 else None)
             if t == 0:
                 nc.vector.tensor_copy(h[:], h_tab[t][:].indirect(offsets[:]))
             else:
                 nc.scalar.activation(h[:], h_tab[t][:].indirect(offsets[:]), ACT.Copy)
             return h
-
-        scalings = [scaling(0, gather_h(0))]
 
         g_codes = tile("g_codes", [P, SLOTS], U32)
         g_scales = tile("g_scales", [P, SLOTS], U8)
@@ -148,11 +153,22 @@ def tile_attend_gsophia_pl_kernel(tc, xT, G, mT, hT, offs, out_0, out_1, out_2, 
                 start=True,
                 stop=True,
             )
-            dw = tile("dw%d" % t, [P, SLOTS], F32)
-            nc.scalar.activation(dw[:], acc[:], ACT.Copy, scale=1.0 / DECAY)
-            return dw
+            return acc
 
-        dws = [gradient(t) for t in range(LANES)]
+        def evacuate(t):
+            if t < 2:
+                dw = dw_early[:, t * SLOTS : (t + 1) * SLOTS]
+                nc.vector.tensor_scalar(dw, accs[t][:], 1.0 / DECAY, None, ALU.mult)
+                return dw
+            dw = tile("dw%d" % t, [P, SLOTS], F32, tag="total%d" % (t - 2))
+            nc.scalar.activation(dw[:], accs[t][:], ACT.Copy, scale=1.0 / DECAY)
+            return dw[:]
+
+        accs = [gradient(t) for t in range(LANES)]
+        scalings = [scaling(0, gather_h(0))]
+        up_win.append(window("up_win1", nc.gpsimd, "x_grouped2"))
+        dw_early = tile("dw_early", [P, 2 * SLOTS], F32, tag="h_tab0")
+        dws = [evacuate(0), evacuate(1)]
 
         def gather_m(t):
             total = tile("total%d" % t, [P, SLOTS], F32)
@@ -164,8 +180,7 @@ def tile_attend_gsophia_pl_kernel(tc, xT, G, mT, hT, offs, out_0, out_1, out_2, 
             win = nm_win[t % NM_WINDOWS]
             for cols in halves:
                 nc.scalar.activation(win[:].indirect(entries(cols)), total[:, cols], ACT.Copy, scale=DECAY)
-            queue = nc.scalar if t + NM_WINDOWS < LANES else nc.sync
-            queue.dma_start(out=nm_rows[t], in_=win[:])
+            nc.scalar.dma_start(out=nm_rows[t], in_=win[:])
 
         def step(t, total):
             inv, sign = scalings[t]
@@ -175,6 +190,8 @@ def tile_attend_gsophia_pl_kernel(tc, xT, G, mT, hT, offs, out_0, out_1, out_2, 
             cut = tile("cut%d" % t, [P, SLOTS], F32)
             for cols in halves:
                 nc.vector.tensor_scalar(cut[:, cols], quotient[:, cols], 1.0, -1.0, ALU.min, ALU.max)
+            if t == 0:
+                up_win.append(window("up_win2", nc.gpsimd, "ratio0"))
             win = up_win[t % UP_WINDOWS]
             nc.vector.tensor_tensor(win[:].indirect(offsets[:]), cut[:], sign[:], ALU.mult)
             nc.sync.dma_start(out=up_rows[t], in_=win[:])
@@ -183,10 +200,11 @@ def tile_attend_gsophia_pl_kernel(tc, xT, G, mT, hT, offs, out_0, out_1, out_2, 
 
         def round_up(t, c):
             win = up_win[t % UP_WINDOWS]
-            nc.vector.tensor_copy(pairs[c][:, t // 2, :, t % 2], win[:, c * CHUNK : (c + 1) * CHUNK])
+            copy = nc.scalar.copy if c >= CHUNKS - 1 - t // 2 else nc.vector.tensor_copy
+            copy(pairs[c][:, t // 2, :, t % 2], win[:, c * CHUNK : (c + 1) * CHUNK])
 
         def weave(c, copy):
-            woven = tile("woven%d" % c, [P, CHUNK * LANES], BF16, tag="h_tab%d" % c)
+            woven = tile("woven%d" % c, [P, CHUNK * LANES], BF16, tag="m_tab%d" % c)
             copy(
                 woven[:].bitcast(WORD[c]).rearrange("p (c u) -> p c u", u=2),
                 pairs[c][:].rearrange("p u c e -> p u (c e)").bitcast(WORD[c]).rearrange("p u c -> p c u"),
@@ -207,12 +225,17 @@ def tile_attend_gsophia_pl_kernel(tc, xT, G, mT, hT, offs, out_0, out_1, out_2, 
                 scalings.append(scaling(t + 1, gather_h(t + 1)))
             step(t, total)
             scatter_nm(t, total)
-            for c in range(CHUNKS):
+            if t < 2:
+                dws.append(evacuate(t + 2))
+            for c in range(CHUNKS if t + 1 < LANES else 2):
                 round_up(t, c)
 
-        wovens = [weave(c, nc.scalar.copy if c < 2 else nc.vector.tensor_copy) for c in range(CHUNKS)]
+        wovens = [weave(c, nc.vector.tensor_copy) for c in range(2)]
+        for c in range(2, CHUNKS):
+            round_up(LANES - 1, c)
+            wovens.append(weave(c, nc.scalar.copy))
         y_scales = tile("y_scales", [P, COLS], U8)
-        for c in (2, 3, 0, 1):
+        for c in range(CHUNKS):
             quantise_y(c, wovens[c], y_scales)
         for q in range(P // 32):
             nc.scalar.dma_start(

@@ -1,6 +1,7 @@
 from contextlib import ExitStack
 
 import concourse.mybir as mybir
+from concourse.masks import make_identity
 
 F32 = mybir.dt.float32
 BF16 = mybir.dt.bfloat16
@@ -25,9 +26,8 @@ CHUNKS = COLS // CHUNK
 LIST_ROWS = 16
 RUN = 4
 G_PIECES = ((0, 256), (256, 512))
-UP_WINDOWS = 3
+UP_WINDOWS = 4
 NM_WINDOWS = 2
-WORD = (I32, I32, U32, U32)
 DECAY = 0.9
 EPS = 0.001
 
@@ -49,54 +49,42 @@ def tile_attend_gsophia_pl_kernel(tc, xT, G, mT, hT, offs, out_0, out_1, out_2, 
         up_rows = out_0.rearrange("(p t) c -> t p c", t=LANES)
         nm_rows = out_1.rearrange("(p t) c -> t p c", t=LANES)
 
-        offsets = sb.tile([P, SLOTS // LIST_ROWS], U16, name="offsets")
-        nc.sync.dma_start(offsets[:], offs)
         x_raw = tile("x_raw", [P, LANES, R], F32)
         nc.sync.dma_start(out=x_raw[:], in_=xT.rearrange("(m t) r -> m t r", t=LANES))
         m_tab = [tile("m_tab%d" % t, [P, COLS], F32) for t in range(LANES)]
         h_tab = [tile("h_tab%d" % t, [P, COLS], F32) for t in range(LANES)]
-        g_raw = []
-        for a, (lo, hi) in enumerate(G_PIECES):
-            g_raw.append(tile("g_raw%d" % a, [P, LANES, hi - lo], F32))
-            nc.sync.dma_start(out=g_raw[a][:], in_=g_rows[:, :, lo:hi])
+        g_raw = tile("g_raw", [P, LANES, SLOTS], F32)
+        nc.sync.dma_start(out=g_raw[:], in_=g_rows)
+        offsets = sb.tile([P, SLOTS // LIST_ROWS], U16, name="offsets")
+        nc.sync.dma_start(offsets[:], offs)
         for t in range(LANES):
             nc.sync.dma_start(out=h_tab[t][:], in_=h_rows[t])
             nc.sync.dma_start(out=m_tab[t][:], in_=m_rows[t])
 
         ident = tile("ident", [P, P], F32)
-        zeros = tile("zeros", [P, P], F32, tag="nm_win1")
-        nc.gpsimd.memset(zeros[:], 0.0)
-        nc.gpsimd.affine_select(
-            out=ident[:],
-            in_=zeros[:],
-            compare_op=ALU.not_equal,
-            fill=1.0,
-            base=0,
-            pattern=[[-1, P]],
-            channel_multiplier=1,
-        )
+        make_identity(nc, ident[:])
 
         halves = [slice(a * HALF, (a + 1) * HALF) for a in range(2)]
 
         def entries(cols):
             return offsets[:, cols.start // LIST_ROWS : cols.stop // LIST_ROWS]
 
-        def window(name, engine, tag=None):
-            win = tile(name, [P, COLS], F32, tag=tag)
-            engine.memset(win[:].bitcast(I32), 0)
+        def window(name):
+            win = tile(name, [P, COLS], F32)
+            nc.vector.memset(win[:].bitcast(I32), 0)
             return win
 
-        nm_win = [window("nm_win0", nc.vector), window("nm_win1", nc.gpsimd)]
-        up_win = [window("up_win0", nc.vector)]
+        nm_win = [window("nm_win%d" % a) for a in range(NM_WINDOWS)]
+        up_win = [window("up_win%d" % a) for a in range(LANES)]
 
-        x_bf = tile("x_bf", [P, LANES * R], BF16)
-        nc.vector.tensor_copy(x_bf[:], x_raw[:].rearrange("p t r -> p (t r)"))
-        x_words = x_bf[:].bitcast(F32)
+        x_bf = [tile("x_bf%d" % t, [P, R], BF16) for t in range(LANES)]
+        for t in range(LANES):
+            nc.scalar.copy(x_bf[t][:], x_raw[:, t, :])
         x_grouped = [tile("x_grouped%d" % t, [P, P * LANES], BF16) for t in range(LANES)]
         for t in range(LANES):
             turned = ps.tile([P, 2, P], F32, name="turned%d" % t)
             for u in range(2):
-                nc.tensor.transpose(turned[:, u, :], x_words[:, t * (R // 2) + u : (t + 1) * (R // 2) : 2], ident[:])
+                nc.tensor.transpose(turned[:, u, :], x_bf[t][:].bitcast(F32)[:, u : R // 2 : 2], ident[:])
             nc.scalar.copy(
                 x_grouped[t][:].bitcast(F32).rearrange("p (m u) -> p m u", u=2), turned[:].rearrange("p u m -> p m u")
             )
@@ -112,12 +100,12 @@ def tile_attend_gsophia_pl_kernel(tc, xT, G, mT, hT, offs, out_0, out_1, out_2, 
             inv = tile("inv%d" % t, [P, SLOTS], F32)
             sign = tile("sign%d" % t, [P, SLOTS], F32)
             nc.scalar.activation(root[:], h[:], ACT.Abs_reciprocal_sqrt, scale=1.0 / DECAY, bias=EPS / DECAY)
-            nc.scalar.activation(inv[:], root[:], ACT.Square)
             nc.scalar.activation(sign[:], h[:], ACT.Sign, bias=EPS)
+            nc.scalar.activation(inv[:], root[:], ACT.Square)
             return inv, sign
 
         def gather_h(t):
-            h = tile("h%d" % t, [P, SLOTS], F32, tag="x_grouped3" if t == 0 else None)
+            h = tile("h%d" % t, [P, SLOTS], F32, tag="x_grouped3" if t == 0 else "total%d_0" % (t - 1))
             if t == 0:
                 nc.vector.tensor_copy(h[:], h_tab[t][:].indirect(offsets[:]))
             else:
@@ -126,18 +114,19 @@ def tile_attend_gsophia_pl_kernel(tc, xT, G, mT, hT, offs, out_0, out_1, out_2, 
 
         g_codes = tile("g_codes", [P, SLOTS], U32)
         g_scales = tile("g_scales", [P, SLOTS], U8)
-        for a, (lo, hi) in enumerate(G_PIECES):
-            g_grouped = tile("g_grouped%d" % a, [P, hi - lo, LANES], BF16)
+        g_grouped = []
+        for a, cols in enumerate(halves):
+            g_grouped.append(tile("g_grouped%d" % a, [P, HALF, LANES], BF16))
             nc.vector.tensor_copy(
-                g_grouped[:].rearrange("p (c i) j -> p c j i", i=RUN),
-                g_raw[a][:].rearrange("p j (c i) -> p c j i", i=RUN),
+                g_grouped[a][:].rearrange("p (c i) j -> p c j i", i=RUN),
+                g_raw[:, :, cols].rearrange("p j (c i) -> p c j i", i=RUN),
             )
-            if a == 0:
-                x_mx = [quantise_x(0)]
+        x_mx = [quantise_x(0)]
+        for a, cols in enumerate(halves):
             nc.vector.quantize_mx(
-                out=g_codes[:, lo:hi].bitcast(E5M2),
-                scales=g_scales[:, lo:hi],
-                in_=g_grouped[:].rearrange("p w j -> p (w j)"),
+                out=g_codes[:, cols].bitcast(E5M2),
+                scales=g_scales[:, cols],
+                in_=g_grouped[a][:].rearrange("p w j -> p (w j)"),
             )
 
         x_mx.extend(quantise_x(t) for t in range(1, LANES))
@@ -160,84 +149,104 @@ def tile_attend_gsophia_pl_kernel(tc, xT, G, mT, hT, offs, out_0, out_1, out_2, 
                 dw = dw_early[:, t * SLOTS : (t + 1) * SLOTS]
                 nc.vector.tensor_scalar(dw, accs[t][:], 1.0 / DECAY, None, ALU.mult)
                 return dw
-            dw = tile("dw%d" % t, [P, SLOTS], F32, tag="total%d" % (t - 2))
+            dw = tile("dw%d" % t, [P, SLOTS], F32, tag="root%d" % (t - 1))
             nc.scalar.activation(dw[:], accs[t][:], ACT.Copy, scale=1.0 / DECAY)
             return dw[:]
 
         accs = [gradient(t) for t in range(LANES)]
         scalings = [scaling(0, gather_h(0))]
-        up_win.append(window("up_win1", nc.gpsimd, "x_grouped2"))
         dw_early = tile("dw_early", [P, 2 * SLOTS], F32, tag="h_tab0")
-        dws = [evacuate(0), evacuate(1)]
+        dws = [evacuate(0)]
 
         def gather_m(t):
-            total = tile("total%d" % t, [P, SLOTS], F32)
-            for cols in halves:
-                nc.vector.tensor_tensor(total[:, cols], m_tab[t][:].indirect(entries(cols)), dws[t][:, cols], ALU.add)
+            total = [tile("total%d_%d" % (t, a), [P, HALF], F32) for a in range(2)]
+            for a, cols in enumerate(halves):
+                nc.vector.tensor_tensor(total[a][:], m_tab[t][:].indirect(entries(cols)), dws[t][:, cols], ALU.add)
             return total
 
-        def scatter_nm(t, total):
+        def scatter_nm(t, total, a):
             win = nm_win[t % NM_WINDOWS]
-            for cols in halves:
-                nc.scalar.activation(win[:].indirect(entries(cols)), total[:, cols], ACT.Copy, scale=DECAY)
-            nc.scalar.dma_start(out=nm_rows[t], in_=win[:])
+            nc.scalar.activation(win[:].indirect(entries(halves[a])), total[a][:], ACT.Copy, scale=DECAY)
+            if a == 1:
+                nc.scalar.dma_start(out=nm_rows[t], in_=win[:])
 
         def step(t, total):
             inv, sign = scalings[t]
             quotient = tile("ratio%d" % t, [P, SLOTS], F32)
-            for cols in halves:
-                nc.vector.tensor_tensor(quotient[:, cols], total[:, cols], inv[:, cols], ALU.mult)
+            for a, cols in enumerate(halves):
+                nc.vector.tensor_tensor(quotient[:, cols], total[a][:], inv[:, cols], ALU.mult)
             cut = tile("cut%d" % t, [P, SLOTS], F32)
-            for cols in halves:
-                nc.vector.tensor_scalar(cut[:, cols], quotient[:, cols], 1.0, -1.0, ALU.min, ALU.max)
-            if t == 0:
-                up_win.append(window("up_win2", nc.gpsimd, "ratio0"))
+            nc.vector.tensor_scalar(cut[:], quotient[:], 1.0, -1.0, ALU.min, ALU.max)
             win = up_win[t % UP_WINDOWS]
             nc.vector.tensor_tensor(win[:].indirect(offsets[:]), cut[:], sign[:], ALU.mult)
             nc.sync.dma_start(out=up_rows[t], in_=win[:])
 
-        pairs = [tile("pairs%d" % c, [P, 2, CHUNK, 2], BF16) for c in range(CHUNKS)]
+        pairs_vector = tile("pairs_vector", [P, 2, 2 * CHUNK, 2], BF16)
+        pairs_third = tile("pairs_third", [P, 2, CHUNK, 2], BF16)
 
-        def round_up(t, c):
-            win = up_win[t % UP_WINDOWS]
-            copy = nc.scalar.copy if c >= CHUNKS - 1 - t // 2 else nc.vector.tensor_copy
-            copy(pairs[c][:, t // 2, :, t % 2], win[:, c * CHUNK : (c + 1) * CHUNK])
+        def round_up(copy, t, pairs, lo, hi):
+            copy(pairs[:, t // 2, :, t % 2], up_win[t][:, lo * CHUNK : hi * CHUNK])
 
-        def weave(c, copy):
-            woven = tile("woven%d" % c, [P, CHUNK * LANES], BF16, tag="m_tab%d" % c)
+        def round_on_vector(t):
+            round_up(nc.vector.tensor_copy, t, pairs_third, 2, 3)
+            for c in range(2):
+                round_up(nc.vector.tensor_copy, t, pairs_vector[:, :, c * CHUNK : (c + 1) * CHUNK, :], c, c + 1)
+
+        def weave(copy, word, woven, pairs):
             copy(
-                woven[:].bitcast(WORD[c]).rearrange("p (c u) -> p c u", u=2),
-                pairs[c][:].rearrange("p u c e -> p u (c e)").bitcast(WORD[c]).rearrange("p u c -> p c u"),
+                woven.bitcast(word).rearrange("p (c u) -> p c u", u=2),
+                pairs.rearrange("p u c e -> p u (c e)").bitcast(word).rearrange("p u c -> p c u"),
             )
             return woven
 
-        def quantise_y(c, woven, y_scales):
-            cols = slice(c * CHUNK, (c + 1) * CHUNK)
-            codes = tile("y_codes%d" % c, [P, CHUNK], U32)
-            nc.vector.quantize_mx(out=codes[:].bitcast(E4M3), scales=y_scales[:, cols], in_=woven[:])
+        def store_words(cols):
             nc.sync.dma_start(
-                out=out_2[0, :, cols, :].rearrange("p c l -> p (c l)").bitcast(I32), in_=codes[:].bitcast(I32)
+                out=out_2[0, :, cols, :].rearrange("p c l -> p (c l)").bitcast(I32), in_=y_codes[:, cols].bitcast(I32)
             )
 
+        totals = [gather_m(0)]
+        last = LANES - 1
         for t in range(LANES):
-            total = gather_m(t)
-            if t + 1 < LANES:
-                scalings.append(scaling(t + 1, gather_h(t + 1)))
-            step(t, total)
-            scatter_nm(t, total)
-            if t < 2:
-                dws.append(evacuate(t + 2))
-            for c in range(CHUNKS if t + 1 < LANES else 2):
-                round_up(t, c)
+            scatter_nm(t, totals[t], 0)
+            step(t, totals[t])
+            if t == 0:
+                dws.append(evacuate(1))
+            else:
+                round_on_vector(t - 1)
+            if t < last:
+                h = gather_h(t + 1)
+            scatter_nm(t, totals[t], 1)
+            if t < last:
+                scalings.append(scaling(t + 1, h))
+                if t + 2 < LANES:
+                    dws.append(evacuate(t + 2))
+                totals.append(gather_m(t + 1))
+        round_on_vector(last)
+        pairs_scalar = tile("pairs_scalar", [P, 2, CHUNK, 2], BF16, tag="total3_1")
+        for t in range(LANES):
+            round_up(nc.scalar.copy, t, pairs_scalar, 3, 4)
 
-        wovens = [weave(c, nc.vector.tensor_copy) for c in range(2)]
-        for c in range(2, CHUNKS):
-            round_up(LANES - 1, c)
-            wovens.append(weave(c, nc.scalar.copy))
-        y_scales = tile("y_scales", [P, COLS], U8)
+        woven = [tile("woven%d" % c, [P, CHUNK * LANES], BF16, tag="h_tab%d" % c) for c in range(1, CHUNKS)]
+        woven.insert(0, tile("woven0", [P, CHUNK * LANES], BF16, tag="m_tab0"))
+        wovens = [
+            weave(nc.vector.tensor_copy, I32, woven[0][:], pairs_vector[:, :, 0:CHUNK, :]),
+            weave(nc.vector.tensor_copy, I32, woven[1][:], pairs_vector[:, :, CHUNK : 2 * CHUNK, :]),
+        ]
+        wovens.append(weave(nc.scalar.copy, U32, woven[2][:], pairs_third[:]))
+        wovens.append(weave(nc.scalar.copy, U32, woven[3][:], pairs_scalar[:]))
+        y_codes = tile("y_codes", [P, COLS], U32, tag="m_tab1")
+        y_scales = tile("y_scales", [P, 2 * CHUNK], U8)
         for c in range(CHUNKS):
-            quantise_y(c, wovens[c], y_scales)
+            cols = slice(c * CHUNK, (c + 1) * CHUNK)
+            nc.vector.quantize_mx(
+                out=y_codes[:, cols].bitcast(E4M3),
+                scales=y_scales[4 * (c // 2) : P, (c % 2) * CHUNK : (c % 2 + 1) * CHUNK],
+                in_=wovens[c],
+            )
+            if c > 0:
+                store_words(cols if c > 1 else slice(0, 2 * CHUNK))
         for q in range(P // 32):
             nc.scalar.dma_start(
-                out=out_3[0, 4 * q : 4 * q + 4, :].bitcast(I32), in_=y_scales[32 * q : 32 * q + 4, :].bitcast(I32)
+                out=out_3[0, 4 * q : 4 * q + 4, :].rearrange("r (a c) -> a r c", a=2).bitcast(I32),
+                in_=y_scales[32 * q : 32 * q + 8, :].bitcast(I32),
             )

@@ -69,13 +69,13 @@ def tile_attend_gsophia_pl_kernel(tc, xT, G, mT, hT, offs, out_0, out_1, out_2, 
         def entries(cols):
             return offsets[:, cols.start // LIST_ROWS : cols.stop // LIST_ROWS]
 
-        def window(name):
-            win = tile(name, [P, COLS], F32)
-            nc.vector.memset(win[:].bitcast(I32), 0)
+        def window(name, engine, tag=None):
+            win = tile(name, [P, COLS], F32, tag=tag)
+            engine.memset(win[:].bitcast(I32), 0)
             return win
 
-        nm_win = [window("nm_win%d" % a) for a in range(NM_WINDOWS)]
-        up_win = [window("up_win%d" % a) for a in range(LANES)]
+        nm_win = [window("nm_win%d" % a, nc.vector) for a in range(NM_WINDOWS)]
+        up_win = [window("up_win%d" % a, nc.vector) for a in range(2)]
 
         x_bf = [tile("x_bf%d" % t, [P, R], BF16) for t in range(LANES)]
         for t in range(LANES):
@@ -176,7 +176,10 @@ def tile_attend_gsophia_pl_kernel(tc, xT, G, mT, hT, offs, out_0, out_1, out_2, 
             for a, cols in enumerate(halves):
                 nc.vector.tensor_tensor(quotient[:, cols], total[a][:], inv[:, cols], ALU.mult)
             cut = tile("cut%d" % t, [P, SLOTS], F32)
-            nc.vector.tensor_scalar(cut[:], quotient[:], 1.0, -1.0, ALU.min, ALU.max)
+            for cols in halves:
+                nc.vector.tensor_scalar(cut[:, cols], quotient[:, cols], 1.0, -1.0, ALU.min, ALU.max)
+            if t < 2:
+                up_win.append(window("up_win%d" % (t + 2), nc.gpsimd, "ratio%d" % t))
             win = up_win[t % UP_WINDOWS]
             nc.vector.tensor_tensor(win[:].indirect(offsets[:]), cut[:], sign[:], ALU.mult)
             nc.sync.dma_start(out=up_rows[t], in_=win[:])

@@ -49,8 +49,9 @@ def tile_attend_gsophia_pl_kernel(tc, xT, G, mT, hT, offs, out_0, out_1, out_2, 
         up_rows = out_0.rearrange("(p t) c -> t p c", t=LANES)
         nm_rows = out_1.rearrange("(p t) c -> t p c", t=LANES)
 
-        x_raw = tile("x_raw", [P, LANES, R], F32)
-        nc.sync.dma_start(out=x_raw[:], in_=xT.rearrange("(m t) r -> m t r", t=LANES))
+        x_rows = xT.rearrange("(m t) r -> m t r", t=LANES)
+        x_raw = [tile("x_raw%d" % a, [P, 2, R], F32) for a in range(2)]
+        nc.sync.dma_start(out=x_raw[0][:], in_=x_rows[:, 0:2, :])
         m_tab = [tile("m_tab%d" % t, [P, COLS], F32) for t in range(LANES)]
         h_tab = [tile("h_tab%d" % t, [P, COLS], F32) for t in range(LANES)]
         g_raw = tile("g_raw", [P, LANES, SLOTS], F32)
@@ -60,6 +61,8 @@ def tile_attend_gsophia_pl_kernel(tc, xT, G, mT, hT, offs, out_0, out_1, out_2, 
         for t in range(LANES):
             nc.sync.dma_start(out=h_tab[t][:], in_=h_rows[t])
             nc.sync.dma_start(out=m_tab[t][:], in_=m_rows[t])
+            if t == 0:
+                nc.sync.dma_start(out=x_raw[1][:], in_=x_rows[:, 2:LANES, :])
 
         ident = tile("ident", [P, P], F32)
         make_identity(nc, ident[:])
@@ -77,23 +80,23 @@ def tile_attend_gsophia_pl_kernel(tc, xT, G, mT, hT, offs, out_0, out_1, out_2, 
         nm_win = [window("nm_win%d" % a, nc.vector) for a in range(NM_WINDOWS)]
         up_win = [window("up_win%d" % a, nc.vector) for a in range(2)]
 
-        x_bf = [tile("x_bf%d" % t, [P, R], BF16) for t in range(LANES)]
-        for t in range(LANES):
-            nc.scalar.copy(x_bf[t][:], x_raw[:, t, :])
-        x_grouped = [tile("x_grouped%d" % t, [P, P * LANES], BF16) for t in range(LANES)]
-        for t in range(LANES):
-            turned = ps.tile([P, 2, P], F32, name="turned%d" % t)
-            for u in range(2):
-                nc.tensor.transpose(turned[:, u, :], x_bf[t][:].bitcast(F32)[:, u : R // 2 : 2], ident[:])
-            nc.scalar.copy(
-                x_grouped[t][:].bitcast(F32).rearrange("p (m u) -> p m u", u=2), turned[:].rearrange("p u m -> p m u")
-            )
+        def turn_x(t, grouped):
+            turned = ps.tile([P, LANES, P], F32, name="turned%d" % t)
+            for j in range(LANES):
+                nc.tensor.transpose(turned[:, j, :], x_raw[t // 2][:, t % 2, j:R:LANES], ident[:])
+            nc.scalar.copy(grouped.rearrange("p (m j) -> p m j", j=LANES), turned[:].rearrange("p j m -> p m j"))
 
-        def quantise_x(t):
-            codes = tile("x_codes%d" % t, [P, P], U32)
-            scales = tile("x_scales%d" % t, [P, P], U8)
-            nc.vector.quantize_mx(out=codes[:].bitcast(E4M3), scales=scales[:], in_=x_grouped[t][:])
-            return codes, scales
+        def group_x(a, tag):
+            grouped = tile("x_grouped%d" % a, [P, 2 * R], BF16, tag=tag)
+            for i in range(2):
+                turn_x(2 * a + i, grouped[:, i * R : (i + 1) * R])
+            return grouped
+
+        def quantise_x(a, grouped, codes_tag):
+            codes = tile("x_codes%d" % a, [P, 2 * P], U32, tag=codes_tag)
+            scales = tile("x_scales%d" % a, [P, 2 * P], U8)
+            nc.vector.quantize_mx(out=codes[:].bitcast(E4M3), scales=scales[:], in_=grouped[:])
+            return [(codes[:, i * P : (i + 1) * P], scales[:, i * P : (i + 1) * P]) for i in range(2)]
 
         def scaling(t, h):
             root = tile("root%d" % t, [P, SLOTS], F32)
@@ -105,7 +108,7 @@ def tile_attend_gsophia_pl_kernel(tc, xT, G, mT, hT, offs, out_0, out_1, out_2, 
             return inv, sign
 
         def gather_h(t):
-            h = tile("h%d" % t, [P, SLOTS], F32, tag="x_grouped3" if t == 0 else "total%d_0" % (t - 1))
+            h = tile("h%d" % t, [P, SLOTS], F32, tag="x_grouped0" if t == 0 else "total%d_0" % (t - 1))
             if t == 0:
                 nc.vector.tensor_copy(h[:], h_tab[t][:].indirect(offsets[:]))
             else:
@@ -121,7 +124,7 @@ def tile_attend_gsophia_pl_kernel(tc, xT, G, mT, hT, offs, out_0, out_1, out_2, 
                 g_grouped[a][:].rearrange("p (c i) j -> p c j i", i=RUN),
                 g_raw[:, :, cols].rearrange("p j (c i) -> p c j i", i=RUN),
             )
-        x_mx = [quantise_x(0)]
+        x_mx = quantise_x(0, group_x(0, None), None)
         for a, cols in enumerate(halves):
             nc.vector.quantize_mx(
                 out=g_codes[:, cols].bitcast(E5M2),
@@ -129,14 +132,12 @@ def tile_attend_gsophia_pl_kernel(tc, xT, G, mT, hT, offs, out_0, out_1, out_2, 
                 in_=g_grouped[a][:].rearrange("p w j -> p (w j)"),
             )
 
-        x_mx.extend(quantise_x(t) for t in range(1, LANES))
-
         def gradient(t):
             acc = ps.tile([P, SLOTS], F32, name="acc%d" % t)
             nc.tensor.matmul_mx(
                 out=acc[:],
-                lhsT=x_mx[t][0][:].bitcast(E4M3),
-                lhsT_scale=x_mx[t][1][:],
+                lhsT=x_mx[t][0].bitcast(E4M3),
+                lhsT_scale=x_mx[t][1],
                 rhs=g_codes[:].bitcast(E5M2),
                 rhs_scale=g_scales[:],
                 start=True,
@@ -149,11 +150,12 @@ def tile_attend_gsophia_pl_kernel(tc, xT, G, mT, hT, offs, out_0, out_1, out_2, 
                 dw = dw_early[:, t * SLOTS : (t + 1) * SLOTS]
                 nc.vector.tensor_scalar(dw, accs[t][:], 1.0 / DECAY, None, ALU.mult)
                 return dw
-            dw = tile("dw%d" % t, [P, SLOTS], F32, tag="root%d" % (t - 1))
+            dw = tile("dw%d" % t, [P, SLOTS], F32, tag=None if t == 2 else "root2")
             nc.scalar.activation(dw[:], accs[t][:], ACT.Copy, scale=1.0 / DECAY)
             return dw[:]
 
-        accs = [gradient(t) for t in range(LANES)]
+        late_x = []
+        accs = [gradient(t) for t in range(2)]
         scalings = [scaling(0, gather_h(0))]
         dw_early = tile("dw_early", [P, 2 * SLOTS], F32, tag="h_tab0")
         dws = [evacuate(0)]
@@ -178,6 +180,10 @@ def tile_attend_gsophia_pl_kernel(tc, xT, G, mT, hT, offs, out_0, out_1, out_2, 
             cut = tile("cut%d" % t, [P, SLOTS], F32)
             for cols in halves:
                 nc.vector.tensor_scalar(cut[:, cols], quotient[:, cols], 1.0, -1.0, ALU.min, ALU.max)
+            if t == 1:
+                x_mx.extend(quantise_x(1, late_x[0], "inv1"))
+                accs.extend(gradient(s) for s in range(2, LANES))
+                dws.append(evacuate(2))
             if t < 2:
                 up_win.append(window("up_win%d" % (t + 2), nc.gpsimd, "ratio%d" % t))
             win = up_win[t % UP_WINDOWS]
@@ -221,8 +227,10 @@ def tile_attend_gsophia_pl_kernel(tc, xT, G, mT, hT, offs, out_0, out_1, out_2, 
             scatter_nm(t, totals[t], 1)
             if t < last:
                 scalings.append(scaling(t + 1, h))
-                if t + 2 < LANES:
-                    dws.append(evacuate(t + 2))
+                if t == 0:
+                    late_x.append(group_x(1, "total0_0"))
+                if t == 1:
+                    dws.append(evacuate(3))
                 totals.append(gather_m(t + 1))
         round_on_vector(last)
         pairs_scalar = tile("pairs_scalar", [P, 2, CHUNK, 2], BF16, tag="total3_1")

@@ -146,18 +146,17 @@ def tile_attend_gsophia_pl_kernel(tc, xT, G, mT, hT, offs, out_0, out_1, out_2, 
             return acc
 
         def evacuate(t):
+            dw = tile("dw%d" % t, [P, SLOTS], F32, tag=(None, "inv0", None, "root2")[t])
             if t < 2:
-                dw = dw_early[:, t * SLOTS : (t + 1) * SLOTS]
-                nc.vector.tensor_scalar(dw, accs[t][:], 1.0 / DECAY, None, ALU.mult)
-                return dw
-            dw = tile("dw%d" % t, [P, SLOTS], F32, tag=None if t == 2 else "root2")
-            nc.scalar.activation(dw[:], accs[t][:], ACT.Copy, scale=1.0 / DECAY)
-            return dw[:]
+                nc.vector.tensor_scalar(dw[:], accs[t][:], 1.0 / DECAY, None, ALU.mult)
+            else:
+                nc.scalar.activation(dw[:], accs[t][:], ACT.Copy, scale=1.0 / DECAY)
+            return dw
 
         late_x = []
         accs = [gradient(t) for t in range(2)]
         scalings = [scaling(0, gather_h(0))]
-        dw_early = tile("dw_early", [P, 2 * SLOTS], F32, tag="h_tab0")
+        up_win.append(window("up_win2", nc.gpsimd, "h_tab0"))
         dws = [evacuate(0)]
 
         def gather_m(t):
@@ -184,8 +183,9 @@ def tile_attend_gsophia_pl_kernel(tc, xT, G, mT, hT, offs, out_0, out_1, out_2, 
                 x_mx.extend(quantise_x(1, late_x[0], "inv1"))
                 accs.extend(gradient(s) for s in range(2, LANES))
                 dws.append(evacuate(2))
-            if t < 2:
-                up_win.append(window("up_win%d" % (t + 2), nc.gpsimd, "ratio%d" % t))
+            if t == 0:
+                up_win.append(window("up_win3", nc.gpsimd, "ratio0"))
+                dws.append(evacuate(1))
             win = up_win[t % UP_WINDOWS]
             nc.vector.tensor_tensor(win[:].indirect(offsets[:]), cut[:], sign[:], ALU.mult)
             nc.sync.dma_start(out=up_rows[t], in_=win[:])
@@ -218,9 +218,7 @@ def tile_attend_gsophia_pl_kernel(tc, xT, G, mT, hT, offs, out_0, out_1, out_2, 
         for t in range(LANES):
             scatter_nm(t, totals[t], 0)
             step(t, totals[t])
-            if t == 0:
-                dws.append(evacuate(1))
-            else:
+            if t > 0:
                 round_on_vector(t - 1)
             if t < last:
                 h = gather_h(t + 1)

@@ -60,9 +60,9 @@ def tile_attend_gsophia_pl_kernel(tc, xT, G, mT, hT, offs, out_0, out_1, out_2, 
         nc.sync.dma_start(offsets[:], offs)
         for t in range(LANES):
             nc.sync.dma_start(out=h_tab[t][:], in_=h_rows[t])
-            nc.sync.dma_start(out=m_tab[t][:], in_=m_rows[t])
-            if t == 0:
+            if t == 1:
                 nc.sync.dma_start(out=x_raw[1][:], in_=x_rows[:, 2:LANES, :])
+            nc.sync.dma_start(out=m_tab[t][:], in_=m_rows[t])
 
         ident = tile("ident", [P, P], F32)
         make_identity(nc, ident[:])
@@ -160,7 +160,11 @@ def tile_attend_gsophia_pl_kernel(tc, xT, G, mT, hT, offs, out_0, out_1, out_2, 
         dws = [evacuate(0)]
 
         def gather_m(t):
-            total = [tile("total%d_%d" % (t, a), [P, HALF], F32) for a in range(2)]
+            if t == LANES - 1:
+                whole = tile("total3", [P, SLOTS], F32, tag="ratio2")
+                total = [whole[:, cols] for cols in halves]
+            else:
+                total = [tile("total%d_%d" % (t, a), [P, HALF], F32) for a in range(2)]
             for a, cols in enumerate(halves):
                 nc.vector.tensor_tensor(total[a][:], m_tab[t][:].indirect(entries(cols)), dws[t][:, cols], ALU.add)
             return total
@@ -231,7 +235,7 @@ def tile_attend_gsophia_pl_kernel(tc, xT, G, mT, hT, offs, out_0, out_1, out_2, 
                     dws.append(evacuate(3))
                 totals.append(gather_m(t + 1))
         round_on_vector(last)
-        pairs_scalar = tile("pairs_scalar", [P, 2, CHUNK, 2], BF16, tag="total3_1")
+        pairs_scalar = tile("pairs_scalar", [P, 2, CHUNK, 2], BF16, tag="ratio2")
         for t in range(LANES):
             round_up(nc.scalar.copy, t, pairs_scalar, 3, 4)
 

@@ -256,8 +256,7 @@ def tile_attend_gsophia_pl_kernel(tc, xT, G, mT, hT, offs, out_0, out_1, out_2, 
                 scales=y_scales[4 * (c // 2) : P, (c % 2) * CHUNK : (c % 2 + 1) * CHUNK],
                 in_=wovens[c],
             )
-            if c > 0:
-                store_words(cols if c > 1 else slice(0, 2 * CHUNK))
+            store_words(cols)
         for q in range(P // 32):
             nc.scalar.dma_start(
                 out=out_3[0, 4 * q : 4 * q + 4, :].rearrange("r (a c) -> a r c", a=2).bitcast(I32),

@@ -27,7 +27,7 @@ LIST_ROWS = 16
 RUN = 4
 G_PIECES = ((0, 256), (256, 512))
 UP_WINDOWS = 4
-NM_WINDOWS = 2
+NM_WINDOWS = 3
 DECAY = 0.9
 EPS = 0.001
 
@@ -77,7 +77,7 @@ def tile_attend_gsophia_pl_kernel(tc, xT, G, mT, hT, offs, out_0, out_1, out_2, 
             engine.memset(win[:].bitcast(I32), 0)
             return win
 
-        nm_win = [window("nm_win%d" % a, nc.vector) for a in range(NM_WINDOWS)]
+        nm_win = [window("nm_win%d" % a, nc.vector) for a in range(2)]
         up_win = [window("up_win%d" % a, nc.vector) for a in range(2)]
 
         def turn_x(t, grouped):
@@ -108,7 +108,7 @@ def tile_attend_gsophia_pl_kernel(tc, xT, G, mT, hT, offs, out_0, out_1, out_2, 
             return inv, sign
 
         def gather_h(t):
-            h = tile("h%d" % t, [P, SLOTS], F32, tag="x_grouped0" if t == 0 else "total%d_0" % (t - 1))
+            h = tile("h%d" % t, [P, SLOTS], F32, tag=("x_grouped0", "dw0", "inv0", "h_tab2")[t])
             if t == 0:
                 nc.vector.tensor_copy(h[:], h_tab[t][:].indirect(offsets[:]))
             else:
@@ -146,7 +146,7 @@ def tile_attend_gsophia_pl_kernel(tc, xT, G, mT, hT, offs, out_0, out_1, out_2, 
             return acc
 
         def evacuate(t):
-            dw = tile("dw%d" % t, [P, SLOTS], F32, tag=(None, "inv0", None, "root2")[t])
+            dw = tile("dw%d" % t, [P, SLOTS], F32, tag=(None, "inv0", "h_tab2", "root2")[t])
             if t < 2:
                 nc.vector.tensor_scalar(dw[:], accs[t][:], 1.0 / DECAY, None, ALU.mult)
             else:
@@ -173,7 +173,8 @@ def tile_attend_gsophia_pl_kernel(tc, xT, G, mT, hT, offs, out_0, out_1, out_2, 
             win = nm_win[t % NM_WINDOWS]
             nc.scalar.activation(win[:].indirect(entries(halves[a])), total[a][:], ACT.Copy, scale=DECAY)
             if a == 1:
-                nc.scalar.dma_start(out=nm_rows[t], in_=win[:])
+                queue = nc.sync if t < 2 else nc.scalar
+                queue.dma_start(out=nm_rows[t], in_=win[:])
 
         def step(t, total):
             inv, sign = scalings[t]
@@ -186,9 +187,9 @@ def tile_attend_gsophia_pl_kernel(tc, xT, G, mT, hT, offs, out_0, out_1, out_2, 
             if t == 1:
                 x_mx.extend(quantise_x(1, late_x[0], "inv1"))
                 accs.extend(gradient(s) for s in range(2, LANES))
-                dws.append(evacuate(2))
+                up_win.append(window("up_win3", nc.gpsimd, "inv1"))
             if t == 0:
-                up_win.append(window("up_win3", nc.gpsimd, "ratio0"))
+                nm_win.append(window("nm_win2", nc.gpsimd, "ratio0"))
                 dws.append(evacuate(1))
             win = up_win[t % UP_WINDOWS]
             nc.vector.tensor_tensor(win[:].indirect(offsets[:]), cut[:], sign[:], ALU.mult)
@@ -222,25 +223,28 @@ def tile_attend_gsophia_pl_kernel(tc, xT, G, mT, hT, offs, out_0, out_1, out_2, 
         for t in range(LANES):
             scatter_nm(t, totals[t], 0)
             step(t, totals[t])
-            if t > 0:
-                round_on_vector(t - 1)
             if t < last:
                 h = gather_h(t + 1)
+                if t == 1:
+                    dws.append(evacuate(2))
+                totals.append(gather_m(t + 1))
+            if t > 0:
+                round_on_vector(t - 1)
             scatter_nm(t, totals[t], 1)
             if t < last:
                 scalings.append(scaling(t + 1, h))
                 if t == 0:
-                    late_x.append(group_x(1, "total0_0"))
+                    late_x.append(group_x(1, "dw0"))
                 if t == 1:
                     dws.append(evacuate(3))
-                totals.append(gather_m(t + 1))
         round_on_vector(last)
-        pairs_scalar = tile("pairs_scalar", [P, 2, CHUNK, 2], BF16, tag="ratio2")
+        late = tile("late", [P, 2 * CHUNK * LANES], BF16, tag="ratio2")
+        pairs_scalar = late[:, 0 : CHUNK * LANES].rearrange("p (u c e) -> p u c e", u=2, e=2)
         for t in range(LANES):
             round_up(nc.scalar.copy, t, pairs_scalar, 3, 4)
 
-        woven = [tile("woven%d" % c, [P, CHUNK * LANES], BF16, tag="h_tab%d" % c) for c in range(1, CHUNKS)]
-        woven.insert(0, tile("woven0", [P, CHUNK * LANES], BF16, tag="m_tab0"))
+        woven = [tile("woven%d" % c, [P, CHUNK * LANES], BF16, tag="h_tab%d" % (c + 1)) for c in range(3)]
+        woven.insert(2, late[:, CHUNK * LANES : 2 * CHUNK * LANES])
         wovens = [
             weave(nc.vector.tensor_copy, I32, woven[0][:], pairs_vector[:, :, 0:CHUNK, :]),
             weave(nc.vector.tensor_copy, I32, woven[1][:], pairs_vector[:, :, CHUNK : 2 * CHUNK, :]),

@@ -15,7 +15,9 @@ ALU = mybir.AluOpType
 ACT = mybir.ActivationFunctionType
 
 P = 128
+QUADRANT = 32
 LANES = 4
+LAST = LANES - 1
 D = 512
 R = 512
 SLOTS = 512
@@ -25,8 +27,7 @@ CHUNK = 512
 CHUNKS = COLS // CHUNK
 LIST_ROWS = 16
 RUN = 4
-G_PIECES = ((0, 256), (256, 512))
-UP_WINDOWS = 4
+X_GROUP = 2
 NM_WINDOWS = 3
 DECAY = 0.9
 EPS = 0.001
@@ -43,26 +44,28 @@ def tile_attend_gsophia_pl_kernel(tc, xT, G, mT, hT, offs, out_0, out_1, out_2, 
         def tile(name, shape, dtype, tag=None):
             return sb.tile(shape, dtype, name=name, tag=tag or name, align_bytes=64)
 
+        x_rows = xT.rearrange("(m t) r -> m t r", t=LANES)
         g_rows = G.rearrange("(p j) w -> p j w", j=LANES)
         m_rows = mT.rearrange("(p t) c -> t p c", t=LANES)
         h_rows = hT.rearrange("(p t) c -> t p c", t=LANES)
         up_rows = out_0.rearrange("(p t) c -> t p c", t=LANES)
         nm_rows = out_1.rearrange("(p t) c -> t p c", t=LANES)
 
-        x_rows = xT.rearrange("(m t) r -> m t r", t=LANES)
-        x_raw = [tile("x_raw%d" % a, [P, 2, R], F32) for a in range(2)]
-        nc.sync.dma_start(out=x_raw[0][:], in_=x_rows[:, 0:2, :])
+        x_raw = [tile("x_raw%d" % a, [P, X_GROUP, R], F32) for a in range(LANES // X_GROUP)]
+        nc.sync.dma_start(out=x_raw[0][:], in_=x_rows[:, 0:X_GROUP, :])
         m_tab = [tile("m_tab%d" % t, [P, COLS], F32) for t in range(LANES)]
         h_tab = [tile("h_tab%d" % t, [P, COLS], F32) for t in range(LANES)]
         g_raw = tile("g_raw", [P, LANES, SLOTS], F32)
         nc.sync.dma_start(out=g_raw[:], in_=g_rows)
         offsets = sb.tile([P, SLOTS // LIST_ROWS], U16, name="offsets")
         nc.sync.dma_start(offsets[:], offs)
-        for t in range(LANES):
+        for t in range(LAST):
             nc.sync.dma_start(out=h_tab[t][:], in_=h_rows[t])
             if t == 1:
-                nc.sync.dma_start(out=x_raw[1][:], in_=x_rows[:, 2:LANES, :])
+                nc.sync.dma_start(out=x_raw[1][:], in_=x_rows[:, X_GROUP:LANES, :])
             nc.sync.dma_start(out=m_tab[t][:], in_=m_rows[t])
+        nc.sync.dma_start(out=m_tab[LAST][:], in_=m_rows[LAST])
+        nc.sync.dma_start(out=h_tab[LAST][:], in_=h_rows[LAST])
 
         ident = tile("ident", [P, P], F32)
         make_identity(nc, ident[:])
@@ -77,26 +80,37 @@ def tile_attend_gsophia_pl_kernel(tc, xT, G, mT, hT, offs, out_0, out_1, out_2, 
             engine.memset(win[:].bitcast(I32), 0)
             return win
 
-        nm_win = [window("nm_win%d" % a, nc.vector) for a in range(2)]
-        up_win = [window("up_win%d" % a, nc.vector) for a in range(2)]
-
-        def turn_x(t, grouped):
-            turned = ps.tile([P, LANES, P], F32, name="turned%d" % t)
-            for j in range(LANES):
-                nc.tensor.transpose(turned[:, j, :], x_raw[t // 2][:, t % 2, j:R:LANES], ident[:])
-            nc.scalar.copy(grouped.rearrange("p (m j) -> p m j", j=LANES), turned[:].rearrange("p j m -> p m j"))
+        nm_win = [window("nm_win%d" % t, nc.vector) for t in range(2)]
+        up_win = [window("up_win%d" % t, nc.vector) for t in range(2)]
 
         def group_x(a, tag):
-            grouped = tile("x_grouped%d" % a, [P, 2 * R], BF16, tag=tag)
-            for i in range(2):
-                turn_x(2 * a + i, grouped[:, i * R : (i + 1) * R])
+            grouped = tile("x_grouped%d" % a, [P, X_GROUP * R], BF16, tag=tag)
+            for i in range(X_GROUP):
+                turned = ps.tile([P, LANES, P], F32, name="turned%d" % (X_GROUP * a + i))
+                for j in range(LANES):
+                    nc.tensor.transpose(turned[:, j, :], x_raw[a][:, i, j:R:LANES], ident[:])
+                nc.scalar.copy(
+                    grouped[:, i * R : (i + 1) * R].rearrange("p (m j) -> p m j", j=LANES),
+                    turned[:].rearrange("p j m -> p m j"),
+                )
             return grouped
 
-        def quantise_x(a, grouped, codes_tag):
-            codes = tile("x_codes%d" % a, [P, 2 * P], U32, tag=codes_tag)
-            scales = tile("x_scales%d" % a, [P, 2 * P], U8)
+        def quantise_x(a, grouped, tag):
+            codes = tile("x_codes%d" % a, [P, X_GROUP * P], U32, tag=tag)
+            scales = tile("x_scales%d" % a, [P, X_GROUP * P], U8)
             nc.vector.quantize_mx(out=codes[:].bitcast(E4M3), scales=scales[:], in_=grouped[:])
-            return [(codes[:, i * P : (i + 1) * P], scales[:, i * P : (i + 1) * P]) for i in range(2)]
+            return [(codes[:, i * P : (i + 1) * P], scales[:, i * P : (i + 1) * P]) for i in range(X_GROUP)]
+
+        dw_tags = ("dw0", "inv0", "h_tab2", "inv2")
+
+        def gather_h(t):
+            if t == 0:
+                h = tile("h0", [P, SLOTS], F32, tag="x_grouped0")
+                nc.vector.tensor_copy(h[:], h_tab[0][:].indirect(offsets[:]))
+                return h
+            h = tile("h%d" % t, [P, SLOTS], F32, tag=dw_tags[t - 1])
+            nc.scalar.activation(h[:], h_tab[t][:].indirect(offsets[:]), ACT.Copy)
+            return h
 
         def scaling(t, h):
             root = tile("root%d" % t, [P, SLOTS], F32)
@@ -106,14 +120,6 @@ def tile_attend_gsophia_pl_kernel(tc, xT, G, mT, hT, offs, out_0, out_1, out_2, 
             nc.scalar.activation(sign[:], h[:], ACT.Sign, bias=EPS)
             nc.scalar.activation(inv[:], root[:], ACT.Square)
             return inv, sign
-
-        def gather_h(t):
-            h = tile("h%d" % t, [P, SLOTS], F32, tag=("x_grouped0", "dw0", "inv0", "h_tab2")[t])
-            if t == 0:
-                nc.vector.tensor_copy(h[:], h_tab[t][:].indirect(offsets[:]))
-            else:
-                nc.scalar.activation(h[:], h_tab[t][:].indirect(offsets[:]), ACT.Copy)
-            return h
 
         g_codes = tile("g_codes", [P, SLOTS], U32)
         g_scales = tile("g_scales", [P, SLOTS], U8)
@@ -132,7 +138,7 @@ def tile_attend_gsophia_pl_kernel(tc, xT, G, mT, hT, offs, out_0, out_1, out_2, 
                 in_=g_grouped[a][:].rearrange("p w j -> p (w j)"),
             )
 
-        def gradient(t):
+        def product(t):
             acc = ps.tile([P, SLOTS], F32, name="acc%d" % t)
             nc.tensor.matmul_mx(
                 out=acc[:],
@@ -145,124 +151,112 @@ def tile_attend_gsophia_pl_kernel(tc, xT, G, mT, hT, offs, out_0, out_1, out_2, 
             )
             return acc
 
-        def evacuate(t):
-            dw = tile("dw%d" % t, [P, SLOTS], F32, tag=(None, "inv0", "h_tab2", "root2")[t])
-            if t < 2:
-                nc.vector.tensor_scalar(dw[:], accs[t][:], 1.0 / DECAY, None, ALU.mult)
-            else:
+        def copy_dw(t):
+            dw = tile("dw%d" % t, [P, SLOTS], F32, tag=dw_tags[t])
+            if t == X_GROUP:
                 nc.scalar.activation(dw[:], accs[t][:], ACT.Copy, scale=1.0 / DECAY)
+            else:
+                nc.vector.tensor_scalar(dw[:], accs[t][:], 1.0 / DECAY, None, ALU.mult)
             return dw
 
-        late_x = []
-        accs = [gradient(t) for t in range(2)]
+        accs = [product(t) for t in range(X_GROUP)]
         scalings = [scaling(0, gather_h(0))]
         up_win.append(window("up_win2", nc.gpsimd, "h_tab0"))
-        dws = [evacuate(0)]
+        dws = [copy_dw(0)]
 
         def gather_m(t):
-            if t == LANES - 1:
-                whole = tile("total3", [P, SLOTS], F32, tag="ratio2")
-                total = [whole[:, cols] for cols in halves]
-            else:
-                total = [tile("total%d_%d" % (t, a), [P, HALF], F32) for a in range(2)]
-            for a, cols in enumerate(halves):
-                nc.vector.tensor_tensor(total[a][:], m_tab[t][:].indirect(entries(cols)), dws[t][:, cols], ALU.add)
+            total = tile("total%d" % t, [P, SLOTS], F32, tag="ratio%d" % (LAST - 1) if t == LAST else None)
+            for cols in halves:
+                nc.vector.tensor_tensor(total[:, cols], m_tab[t][:].indirect(entries(cols)), dws[t][:, cols], ALU.add)
             return total
 
-        def scatter_nm(t, total, a):
+        def scatter_nm(t, cols):
             win = nm_win[t % NM_WINDOWS]
-            nc.scalar.activation(win[:].indirect(entries(halves[a])), total[a][:], ACT.Copy, scale=DECAY)
-            if a == 1:
-                queue = nc.sync if t < 2 else nc.scalar
-                queue.dma_start(out=nm_rows[t], in_=win[:])
+            nc.scalar.activation(win[:].indirect(entries(cols)), totals[t][:, cols], ACT.Copy, scale=DECAY)
+            return win
 
-        def step(t, total):
-            inv, sign = scalings[t]
-            quotient = tile("ratio%d" % t, [P, SLOTS], F32)
-            for a, cols in enumerate(halves):
-                nc.vector.tensor_tensor(quotient[:, cols], total[a][:], inv[:, cols], ALU.mult)
+        def clipped_ratio(t):
+            ratio = tile("ratio%d" % t, [P, SLOTS], F32)
+            for cols in halves:
+                nc.vector.tensor_tensor(ratio[:, cols], totals[t][:, cols], scalings[t][0][:, cols], ALU.mult)
             cut = tile("cut%d" % t, [P, SLOTS], F32)
             for cols in halves:
-                nc.vector.tensor_scalar(cut[:, cols], quotient[:, cols], 1.0, -1.0, ALU.min, ALU.max)
-            if t == 1:
-                x_mx.extend(quantise_x(1, late_x[0], "inv1"))
-                accs.extend(gradient(s) for s in range(2, LANES))
-                up_win.append(window("up_win3", nc.gpsimd, "inv1"))
-            if t == 0:
-                nm_win.append(window("nm_win2", nc.gpsimd, "ratio0"))
-                dws.append(evacuate(1))
-            win = up_win[t % UP_WINDOWS]
-            nc.vector.tensor_tensor(win[:].indirect(offsets[:]), cut[:], sign[:], ALU.mult)
-            nc.sync.dma_start(out=up_rows[t], in_=win[:])
+                nc.vector.tensor_scalar(cut[:, cols], ratio[:, cols], 1.0, -1.0, ALU.min, ALU.max)
+            return cut
 
-        pairs_vector = tile("pairs_vector", [P, 2, 2 * CHUNK, 2], BF16)
-        pairs_third = tile("pairs_third", [P, 2, CHUNK, 2], BF16)
+        def scatter_up(t, cut):
+            nc.vector.tensor_tensor(up_win[t][:].indirect(offsets[:]), cut[:], scalings[t][1][:], ALU.mult)
+            nc.sync.dma_start(out=up_rows[t], in_=up_win[t][:])
 
-        def round_up(copy, t, pairs, lo, hi):
-            copy(pairs[:, t // 2, :, t % 2], up_win[t][:, lo * CHUNK : hi * CHUNK])
+        pairs_01 = tile("pairs_01", [P, 2, 2 * CHUNK, 2], BF16)
+        pairs_2 = tile("pairs_2", [P, 2, CHUNK, 2], BF16)
+        pairs = [pairs_01[:, :, 0:CHUNK, :], pairs_01[:, :, CHUNK : 2 * CHUNK, :], pairs_2[:]]
+
+        def round_up(copy, t, c):
+            copy(pairs[c][:, t // 2, :, t % 2], up_win[t][:, c * CHUNK : (c + 1) * CHUNK])
 
         def round_on_vector(t):
-            round_up(nc.vector.tensor_copy, t, pairs_third, 2, 3)
-            for c in range(2):
-                round_up(nc.vector.tensor_copy, t, pairs_vector[:, :, c * CHUNK : (c + 1) * CHUNK, :], c, c + 1)
-
-        def weave(copy, word, woven, pairs):
-            copy(
-                woven.bitcast(word).rearrange("p (c u) -> p c u", u=2),
-                pairs.rearrange("p u c e -> p u (c e)").bitcast(word).rearrange("p u c -> p c u"),
-            )
-            return woven
-
-        def store_words(cols):
-            nc.sync.dma_start(
-                out=out_2[0, :, cols, :].rearrange("p c l -> p (c l)").bitcast(I32), in_=y_codes[:, cols].bitcast(I32)
-            )
+            for c in (2, 0, 1):
+                round_up(nc.vector.tensor_copy, t, c)
 
         totals = [gather_m(0)]
-        last = LANES - 1
         for t in range(LANES):
-            scatter_nm(t, totals[t], 0)
-            step(t, totals[t])
-            if t < last:
-                h = gather_h(t + 1)
-                if t == 1:
-                    dws.append(evacuate(2))
+            scatter_nm(t, halves[0])
+            cut = clipped_ratio(t)
+            if t == 0:
+                nm_win.append(window("nm_win2", nc.gpsimd, "ratio0"))
+                dws.append(copy_dw(1))
+            if t == 1:
+                x_mx.extend(quantise_x(1, late_x, "inv1"))
+                accs.extend(product(s) for s in range(X_GROUP, LANES))
+                up_win.append(window("up_win3", nc.gpsimd, "inv1"))
+            if t == 2:
+                dws.append(copy_dw(LAST))
+            scatter_up(t, cut)
+            if t < LAST:
+                h_next = gather_h(t + 1)
+                if t + 1 == X_GROUP:
+                    dws.append(copy_dw(X_GROUP))
                 totals.append(gather_m(t + 1))
             if t > 0:
                 round_on_vector(t - 1)
-            scatter_nm(t, totals[t], 1)
-            if t < last:
-                scalings.append(scaling(t + 1, h))
-                if t == 0:
-                    late_x.append(group_x(1, "dw0"))
-                if t == 1:
-                    dws.append(evacuate(3))
-        round_on_vector(last)
-        late = tile("late", [P, 2 * CHUNK * LANES], BF16, tag="ratio2")
-        pairs_scalar = late[:, 0 : CHUNK * LANES].rearrange("p (u c e) -> p u c e", u=2, e=2)
-        for t in range(LANES):
-            round_up(nc.scalar.copy, t, pairs_scalar, 3, 4)
+            nm_done = scatter_nm(t, halves[1])
+            queue = nc.scalar if t == LAST else nc.sync
+            queue.dma_start(out=nm_rows[t], in_=nm_done[:])
+            if t < LAST:
+                scalings.append(scaling(t + 1, h_next))
+            if t == 0:
+                late_x = group_x(1, dw_tags[0])
+        round_on_vector(LAST)
 
-        woven = [tile("woven%d" % c, [P, CHUNK * LANES], BF16, tag="h_tab%d" % (c + 1)) for c in range(3)]
+        late = tile("late", [P, 2 * CHUNK * LANES], BF16, tag="ratio%d" % (LAST - 1))
+        pairs.append(late[:, 0 : CHUNK * LANES].rearrange("p (u c e) -> p u c e", u=2, e=2))
+        for t in range(LANES):
+            round_up(nc.scalar.copy, t, CHUNKS - 1)
+
+        woven = [tile("woven%d" % a, [P, CHUNK * LANES], BF16, tag="h_tab%d" % (a + 1))[:] for a in range(CHUNKS - 1)]
         woven.insert(2, late[:, CHUNK * LANES : 2 * CHUNK * LANES])
-        wovens = [
-            weave(nc.vector.tensor_copy, I32, woven[0][:], pairs_vector[:, :, 0:CHUNK, :]),
-            weave(nc.vector.tensor_copy, I32, woven[1][:], pairs_vector[:, :, CHUNK : 2 * CHUNK, :]),
-        ]
-        wovens.append(weave(nc.scalar.copy, U32, woven[2][:], pairs_third[:]))
-        wovens.append(weave(nc.scalar.copy, U32, woven[3][:], pairs_scalar[:]))
+        for c in range(CHUNKS):
+            copy, word = (nc.vector.tensor_copy, I32) if c < 2 else (nc.scalar.copy, U32)
+            copy(
+                woven[c].bitcast(word).rearrange("p (c u) -> p c u", u=2),
+                pairs[c].rearrange("p u c e -> p u (c e)").bitcast(word).rearrange("p u c -> p c u"),
+            )
+
         y_codes = tile("y_codes", [P, COLS], U32, tag="m_tab1")
         y_scales = tile("y_scales", [P, 2 * CHUNK], U8)
         for c in range(CHUNKS):
             cols = slice(c * CHUNK, (c + 1) * CHUNK)
             nc.vector.quantize_mx(
                 out=y_codes[:, cols].bitcast(E4M3),
-                scales=y_scales[4 * (c // 2) : P, (c % 2) * CHUNK : (c % 2 + 1) * CHUNK],
-                in_=wovens[c],
+                scales=y_scales[LANES * (c // 2) : P, (c % 2) * CHUNK : (c % 2 + 1) * CHUNK],
+                in_=woven[c],
             )
-            store_words(cols)
-        for q in range(P // 32):
+            nc.sync.dma_start(
+                out=out_2[0, :, cols, :].rearrange("p c l -> p (c l)").bitcast(I32), in_=y_codes[:, cols].bitcast(I32)
+            )
+        for q in range(P // QUADRANT):
             nc.scalar.dma_start(
-                out=out_3[0, 4 * q : 4 * q + 4, :].rearrange("r (a c) -> a r c", a=2).bitcast(I32),
-                in_=y_scales[32 * q : 32 * q + 8, :].bitcast(I32),
+                out=out_3[0, LANES * q : LANES * (q + 1), :].rearrange("r (a c) -> a r c", a=2).bitcast(I32),
+                in_=y_scales[QUADRANT * q : QUADRANT * q + 2 * LANES, :].bitcast(I32),
             )

@@ -81,7 +81,7 @@ def tile_attend_gsophia_pl_kernel(tc, xT, G, mT, hT, offs, out_0, out_1, out_2, 
             return win
 
         nm_win = [window("nm_win%d" % t, nc.vector) for t in range(2)]
-        up_win = [window("up_win%d" % t, nc.vector) for t in range(2)]
+        up_win = [window("up_win0", nc.vector)]
 
         def group_x(a, tag):
             grouped = tile("x_grouped%d" % a, [P, X_GROUP * R], BF16, tag=tag)
@@ -161,7 +161,7 @@ def tile_attend_gsophia_pl_kernel(tc, xT, G, mT, hT, offs, out_0, out_1, out_2, 
 
         accs = [product(t) for t in range(X_GROUP)]
         scalings = [scaling(0, gather_h(0))]
-        up_win.append(window("up_win2", nc.gpsimd, "h_tab0"))
+        up_win.append(window("up_win1", nc.gpsimd, "h_tab0"))
         dws = [copy_dw(0)]
 
         def gather_m(t):
@@ -176,12 +176,12 @@ def tile_attend_gsophia_pl_kernel(tc, xT, G, mT, hT, offs, out_0, out_1, out_2, 
             return win
 
         def clipped_ratio(t):
-            ratio = tile("ratio%d" % t, [P, SLOTS], F32)
-            for cols in halves:
-                nc.vector.tensor_tensor(ratio[:, cols], totals[t][:, cols], scalings[t][0][:, cols], ALU.mult)
+            ratio = [tile("ratio%d%s" % (t, "a" * (1 - a)), [P, HALF], F32) for a in range(2)]
+            for a, cols in enumerate(halves):
+                nc.vector.tensor_tensor(ratio[a][:], totals[t][:, cols], scalings[t][0][:, cols], ALU.mult)
             cut = tile("cut%d" % t, [P, SLOTS], F32)
-            for cols in halves:
-                nc.vector.tensor_scalar(cut[:, cols], ratio[:, cols], 1.0, -1.0, ALU.min, ALU.max)
+            for a, cols in enumerate(halves):
+                nc.vector.tensor_scalar(cut[:, cols], ratio[a][:], 1.0, -1.0, ALU.min, ALU.max)
             return cut
 
         def scatter_up(t, cut):
@@ -209,9 +209,10 @@ def tile_attend_gsophia_pl_kernel(tc, xT, G, mT, hT, offs, out_0, out_1, out_2, 
             if t == 1:
                 x_mx.extend(quantise_x(1, late_x, "inv1"))
                 accs.extend(product(s) for s in range(X_GROUP, LANES))
-                up_win.append(window("up_win3", nc.gpsimd, "inv1"))
+                up_win.append(window("up_win2", nc.gpsimd, "inv1"))
             if t == 2:
                 dws.append(copy_dw(LAST))
+                up_win.append(window("up_win3", nc.gpsimd, "ratio2a"))
             scatter_up(t, cut)
             if t < LAST:
                 h_next = gather_h(t + 1)

@@ -81,7 +81,7 @@ def tile_attend_gsophia_pl_kernel(tc, xT, G, mT, hT, offs, out_0, out_1, out_2, 
             return win
 
         nm_win = [window("nm_win%d" % t, nc.vector) for t in range(2)]
-        up_win = [window("up_win0", nc.vector)]
+        up_win = [window("up_win%d" % t, nc.vector) for t in range(2)]
 
         def group_x(a, tag):
             grouped = tile("x_grouped%d" % a, [P, X_GROUP * R], BF16, tag=tag)
@@ -161,7 +161,6 @@ def tile_attend_gsophia_pl_kernel(tc, xT, G, mT, hT, offs, out_0, out_1, out_2, 
 
         accs = [product(t) for t in range(X_GROUP)]
         scalings = [scaling(0, gather_h(0))]
-        up_win.append(window("up_win1", nc.gpsimd, "h_tab0"))
         dws = [copy_dw(0)]
 
         def gather_m(t):
@@ -245,19 +244,25 @@ def tile_attend_gsophia_pl_kernel(tc, xT, G, mT, hT, offs, out_0, out_1, out_2, 
             )
 
         y_codes = tile("y_codes", [P, COLS], U32, tag="m_tab1")
-        y_scales = tile("y_scales", [P, 2 * CHUNK], U8)
-        for c in range(CHUNKS):
-            cols = slice(c * CHUNK, (c + 1) * CHUNK)
-            nc.vector.quantize_mx(
-                out=y_codes[:, cols].bitcast(E4M3),
-                scales=y_scales[LANES * (c // 2) : P, (c % 2) * CHUNK : (c % 2 + 1) * CHUNK],
-                in_=woven[c],
-            )
+        y_scales = tile("y_scales", [P, CHUNK], U8)
+        piece = CHUNK // 2
+
+        def store_words(cols):
             nc.sync.dma_start(
                 out=out_2[0, :, cols, :].rearrange("p c l -> p (c l)").bitcast(I32), in_=y_codes[:, cols].bitcast(I32)
             )
+
+        for c in range(CHUNKS):
+            for a in range(2):
+                cols = slice(c * CHUNK + a * piece, c * CHUNK + (a + 1) * piece)
+                nc.vector.quantize_mx(
+                    out=y_codes[:, cols].bitcast(E4M3),
+                    scales=y_scales[LANES * c : P, a * piece : (a + 1) * piece],
+                    in_=woven[c][:, a * piece * LANES : (a + 1) * piece * LANES],
+                )
+            store_words(slice(c * CHUNK, (c + 1) * CHUNK))
         for q in range(P // QUADRANT):
             nc.scalar.dma_start(
-                out=out_3[0, LANES * q : LANES * (q + 1), :].rearrange("r (a c) -> a r c", a=2).bitcast(I32),
-                in_=y_scales[QUADRANT * q : QUADRANT * q + 2 * LANES, :].bitcast(I32),
+                out=out_3[0, LANES * q : LANES * (q + 1), :].rearrange("r (c x) -> c r x", c=CHUNKS).bitcast(I32),
+                in_=y_scales[QUADRANT * q : QUADRANT * q + CHUNKS * LANES, :].bitcast(I32),
             )

@@ -238,10 +238,14 @@ def tile_attend_gsophia_pl_kernel(tc, xT, G, mT, hT, offs, out_0, out_1, out_2, 
         woven.insert(2, late[:, CHUNK * LANES : 2 * CHUNK * LANES])
         for c in range(CHUNKS):
             copy, word = (nc.vector.tensor_copy, I32) if c < 2 else (nc.scalar.copy, U32)
-            copy(
-                woven[c].bitcast(word).rearrange("p (c u) -> p c u", u=2),
-                pairs[c].rearrange("p u c e -> p u (c e)").bitcast(word).rearrange("p u c -> p c u"),
-            )
+            parts = 2 if c == CHUNKS - 1 else 1
+            width = CHUNK // parts
+            for a in range(parts):
+                cols = slice(a * width, (a + 1) * width)
+                copy(
+                    woven[c].bitcast(word).rearrange("p (c u) -> p c u", u=2)[:, cols, :],
+                    pairs[c].rearrange("p u c e -> p u (c e)").bitcast(word).rearrange("p u c -> p c u")[:, cols, :],
+                )
 
         y_codes = tile("y_codes", [P, COLS], U32, tag="m_tab1")
         y_scales = tile("y_scales", [P, CHUNK], U8)

@@ -29,6 +29,9 @@ LIST_ROWS = 16
 RUN = 4
 X_GROUP = 2
 NM_WINDOWS = 3
+PIECE = CHUNK // 2
+FRONT = 5 * PIECE
+BANKS = (COLS - FRONT) // PIECE
 DECAY = 0.9
 EPS = 0.001
 
@@ -188,14 +191,14 @@ def tile_attend_gsophia_pl_kernel(tc, xT, G, mT, hT, offs, out_0, out_1, out_2, 
             nc.sync.dma_start(out=up_rows[t], in_=up_win[t][:])
 
         pairs_01 = tile("pairs_01", [P, 2, 2 * CHUNK, 2], BF16)
-        pairs_2 = tile("pairs_2", [P, 2, CHUNK, 2], BF16)
+        pairs_2 = tile("pairs_2", [P, 2, PIECE, 2], BF16)
         pairs = [pairs_01[:, :, 0:CHUNK, :], pairs_01[:, :, CHUNK : 2 * CHUNK, :], pairs_2[:]]
 
         def round_up(copy, t, c):
-            copy(pairs[c][:, t // 2, :, t % 2], up_win[t][:, c * CHUNK : (c + 1) * CHUNK])
+            copy(pairs[c][:, t // 2, :, t % 2], up_win[t][:, c * CHUNK : min((c + 1) * CHUNK, FRONT)])
 
         def round_on_vector(t):
-            for c in (2, 0, 1):
+            for c in (0, 1, 2):
                 round_up(nc.vector.tensor_copy, t, c)
 
         totals = [gather_m(0)]
@@ -229,23 +232,46 @@ def tile_attend_gsophia_pl_kernel(tc, xT, G, mT, hT, offs, out_0, out_1, out_2, 
                 late_x = group_x(1, dw_tags[0])
         round_on_vector(LAST)
 
-        late = tile("late", [P, 2 * CHUNK * LANES], BF16, tag="ratio%d" % (LAST - 1))
-        pairs.append(late[:, 0 : CHUNK * LANES].rearrange("p (u c e) -> p u c e", u=2, e=2))
-        for t in range(LANES):
-            round_up(nc.scalar.copy, t, CHUNKS - 1)
+        late = tile("late", [P, 2 * BANKS * PIECE], BF16, tag="ratio%d" % (LAST - 1))
+        woven = [tile("woven%d" % a, [P, CHUNK * LANES], BF16, tag="h_tab%d" % (a + 1))[:] for a in range(2)]
+        woven.append(tile("woven2", [P, PIECE * LANES], BF16, tag="h_tab3")[:])
+        ready = [woven[a // 2][:, a % 2 * PIECE * LANES : (a % 2 + 1) * PIECE * LANES] for a in range(FRONT // PIECE)]
 
-        woven = [tile("woven%d" % a, [P, CHUNK * LANES], BF16, tag="h_tab%d" % (a + 1))[:] for a in range(CHUNKS - 1)]
-        woven.insert(2, late[:, CHUNK * LANES : 2 * CHUNK * LANES])
-        for c in range(CHUNKS):
-            copy, word = (nc.vector.tensor_copy, I32) if c < 2 else (nc.scalar.copy, U32)
-            parts = 2 if c == CHUNKS - 1 else 1
-            width = CHUNK // parts
-            for a in range(parts):
-                cols = slice(a * width, (a + 1) * width)
-                copy(
-                    woven[c].bitcast(word).rearrange("p (c u) -> p c u", u=2)[:, cols, :],
-                    pairs[c].rearrange("p u c e -> p u (c e)").bitcast(word).rearrange("p u c -> p c u")[:, cols, :],
+        def weave(copy, word, c):
+            copy(
+                woven[c].bitcast(word).rearrange("p (c u) -> p c u", u=2),
+                pairs[c].rearrange("p u c e -> p u (c e)").bitcast(word).rearrange("p u c -> p c u"),
+            )
+
+        back = [ps.tile([P, 2, 2, P], F32, name="back%d" % k, tag="acc%d" % k) for k in range(BANKS)]
+        across = []
+        for u in range(2):
+            for k in range(BANKS):
+                bank = ps.tile([P, 2, 2, P], F32, name="over%d%d" % (u, k), tag="turned%d" % k)
+                for e in range(2):
+                    for j in range(2):
+                        at = FRONT + (2 * k + j) * P
+                        nc.tensor.transpose(bank[:, j, e, :], up_win[2 * u + e][:, at : at + P], ident[:])
+                if u == 0:
+                    across.append(late[:, 2 * k * PIECE : 2 * (k + 1) * PIECE])
+                else:
+                    across.append(tile("across%d" % k, [P, 2 * PIECE], BF16)[:])
+                nc.scalar.copy(
+                    across[-1].rearrange("q (j p e) -> q j p e", j=2, e=2), bank[:].rearrange("q j e p -> q j p e")
                 )
+        for k in range(BANKS):
+            for u in range(2):
+                for j in range(2):
+                    words = across[BANKS * u + k].bitcast(F32)
+                    nc.tensor.transpose(back[k][:, j, u, :], words[:, j * P : (j + 1) * P], ident[:])
+        for c in range(3):
+            weave(nc.vector.tensor_copy, I32, c)
+        for k in range(BANKS):
+            ready.append(tile("ready%d" % k, [P, PIECE * LANES], BF16)[:])
+            nc.scalar.copy(
+                ready[-1].bitcast(F32).rearrange("p (j c u) -> p j c u", j=2, u=2),
+                back[k][:].rearrange("p j u c -> p j c u"),
+            )
 
         y_codes = tile("y_codes", [P, COLS], U32, tag="m_tab1")
         y_scales = tile("y_scales", [P, CHUNK], U8)
@@ -262,7 +288,7 @@ def tile_attend_gsophia_pl_kernel(tc, xT, G, mT, hT, offs, out_0, out_1, out_2, 
                 nc.vector.quantize_mx(
                     out=y_codes[:, cols].bitcast(E4M3),
                     scales=y_scales[LANES * c : P, a * piece : (a + 1) * piece],
-                    in_=woven[c][:, a * piece * LANES : (a + 1) * piece * LANES],
+                    in_=ready[2 * c + a],
                 )
             store_words(slice(c * CHUNK, (c + 1) * CHUNK))
         for q in range(P // QUADRANT):

@@ -104,7 +104,7 @@ def tile_attend_gsophia_pl_kernel(tc, xT, G, mT, hT, offs, out_0, out_1, out_2, 
             nc.vector.quantize_mx(out=codes[:].bitcast(E4M3), scales=scales[:], in_=grouped[:])
             return [(codes[:, i * P : (i + 1) * P], scales[:, i * P : (i + 1) * P]) for i in range(X_GROUP)]
 
-        dw_tags = ("dw0", "inv0", "h_tab2", "inv2")
+        dw_tags = ("dw0", "dw1", "h_tab2", "inv2")
 
         def gather_h(t):
             if t == 0:
@@ -164,7 +164,7 @@ def tile_attend_gsophia_pl_kernel(tc, xT, G, mT, hT, offs, out_0, out_1, out_2, 
 
         accs = [product(t) for t in range(X_GROUP)]
         scalings = [scaling(0, gather_h(0))]
-        dws = [copy_dw(0)]
+        dws = [copy_dw(t) for t in range(X_GROUP)]
 
         def gather_m(t):
             total = tile("total%d" % t, [P, SLOTS], F32, tag="ratio%d" % (LAST - 1) if t == LAST else None)
@@ -207,7 +207,6 @@ def tile_attend_gsophia_pl_kernel(tc, xT, G, mT, hT, offs, out_0, out_1, out_2, 
             cut = clipped_ratio(t)
             if t == 0:
                 nm_win.append(window("nm_win2", nc.gpsimd, "ratio0"))
-                dws.append(copy_dw(1))
             if t == 1:
                 x_mx.extend(quantise_x(1, late_x, "inv1"))
                 accs.extend(product(s) for s in range(X_GROUP, LANES))

@@ -112,14 +112,18 @@ def tile_attend_gsophia_pl_kernel(tc, xT, G, mT, hT, offs, out_0, out_1, out_2, 
                 nc.vector.tensor_copy(h[:], h_tab[0][:].indirect(offsets[:]))
                 return h
             h = tile("h%d" % t, [P, SLOTS], F32, tag=dw_tags[t - 1])
-            nc.scalar.activation(h[:], h_tab[t][:].indirect(offsets[:]), ACT.Copy)
+            for cols in halves if t == X_GROUP else [slice(0, SLOTS)]:
+                nc.scalar.activation(h[:, cols], h_tab[t][:].indirect(entries(cols)), ACT.Copy)
             return h
 
         def scaling(t, h):
             root = tile("root%d" % t, [P, SLOTS], F32)
             inv = tile("inv%d" % t, [P, SLOTS], F32)
             sign = tile("sign%d" % t, [P, SLOTS], F32)
-            nc.scalar.activation(root[:], h[:], ACT.Abs_reciprocal_sqrt, scale=1.0 / DECAY, bias=EPS / DECAY)
+            for cols in halves if t == X_GROUP else [slice(0, SLOTS)]:
+                nc.scalar.activation(
+                    root[:, cols], h[:, cols], ACT.Abs_reciprocal_sqrt, scale=1.0 / DECAY, bias=EPS / DECAY
+                )
             nc.scalar.activation(sign[:], h[:], ACT.Sign, bias=EPS)
             nc.scalar.activation(inv[:], root[:], ACT.Square)
             return inv, sign
@@ -222,10 +226,12 @@ def tile_attend_gsophia_pl_kernel(tc, xT, G, mT, hT, offs, out_0, out_1, out_2, 
                 totals.append(gather_m(t + 1))
             if t > 0:
                 round_on_vector(t - 1)
+            if t + 1 == X_GROUP:
+                scalings.append(scaling(t + 1, h_next))
             nm_done = scatter_nm(t, halves[1])
             queue = nc.scalar if t == LAST else nc.sync
             queue.dma_start(out=nm_rows[t], in_=nm_done[:])
-            if t < LAST:
+            if t < LAST and t + 1 != X_GROUP:
                 scalings.append(scaling(t + 1, h_next))
             if t == 0:
                 late_x = group_x(1, dw_tags[0])

from contextlib import ExitStack

import concourse.mybir as mybir
from concourse.masks import make_identity

F32 = mybir.dt.float32
BF16 = mybir.dt.bfloat16
U32 = mybir.dt.uint32
I32 = mybir.dt.int32
U16 = mybir.dt.uint16
U8 = mybir.dt.uint8
E4M3 = mybir.dt.float8_e4m3fn_x4
E5M2 = mybir.dt.float8_e5m2_x4
ALU = mybir.AluOpType
ACT = mybir.ActivationFunctionType

P = 128
QUADRANT = 32
LANES = 4
LAST = LANES - 1
D = 512
R = 512
SLOTS = 512
COLS = 2048
HALF = SLOTS // 2
CHUNK = 512
CHUNKS = COLS // CHUNK
LIST_ROWS = 16
RUN = 4
X_GROUP = 2
NM_WINDOWS = 3
PIECE = CHUNK // 2
FRONT = 5 * PIECE
BANKS = (COLS - FRONT) // PIECE
DECAY = 0.9
EPS = 0.001

FLOPS = 2 * D * R * SLOTS


def tile_attend_gsophia_pl_kernel(tc, xT, G, mT, hT, offs, out_0, out_1, out_2, out_3):
    nc = tc.nc
    with ExitStack() as ctx:
        sb = ctx.enter_context(tc.tile_pool(name="sb", bufs=1))
        ps = ctx.enter_context(tc.psum_pool(name="ps", bufs=1))

        def tile(name, shape, dtype, tag=None):
            return sb.tile(shape, dtype, name=name, tag=tag or name, align_bytes=64)

        x_rows = xT.rearrange("(m t) r -> m t r", t=LANES)
        g_rows = G.rearrange("(p j) w -> p j w", j=LANES)
        m_rows = mT.rearrange("(p t) c -> t p c", t=LANES)
        h_rows = hT.rearrange("(p t) c -> t p c", t=LANES)
        up_rows = out_0.rearrange("(p t) c -> t p c", t=LANES)
        nm_rows = out_1.rearrange("(p t) c -> t p c", t=LANES)

        x_raw = [tile("x_raw%d" % a, [P, X_GROUP, R], F32) for a in range(LANES // X_GROUP)]
        nc.sync.dma_start(out=x_raw[0][:], in_=x_rows[:, 0:X_GROUP, :])
        m_tab = [tile("m_tab%d" % t, [P, COLS], F32) for t in range(LANES)]
        h_tab = [tile("h_tab%d" % t, [P, COLS], F32) for t in range(LANES)]
        g_raw = tile("g_raw", [P, LANES, SLOTS], F32)
        nc.sync.dma_start(out=g_raw[:], in_=g_rows)
        offsets = sb.tile([P, SLOTS // LIST_ROWS], U16, name="offsets")
        nc.sync.dma_start(offsets[:], offs)
        for t in range(LAST):
            nc.sync.dma_start(out=h_tab[t][:], in_=h_rows[t])
            if t == 1:
                nc.sync.dma_start(out=x_raw[1][:], in_=x_rows[:, X_GROUP:LANES, :])
            nc.sync.dma_start(out=m_tab[t][:], in_=m_rows[t])
        nc.sync.dma_start(out=m_tab[LAST][:], in_=m_rows[LAST])
        nc.sync.dma_start(out=h_tab[LAST][:], in_=h_rows[LAST])

        ident = tile("ident", [P, P], F32)
        make_identity(nc, ident[:])

        halves = [slice(a * HALF, (a + 1) * HALF) for a in range(2)]

        def entries(cols):
            return offsets[:, cols.start // LIST_ROWS : cols.stop // LIST_ROWS]

        def window(name, engine, tag=None):
            win = tile(name, [P, COLS], F32, tag=tag)
            engine.memset(win[:].bitcast(I32), 0)
            return win

        nm_win = [window("nm_win%d" % t, nc.vector) for t in range(2)]
        up_win = [window("up_win%d" % t, nc.vector) for t in range(2)]

        def group_x(a, tag):
            grouped = tile("x_grouped%d" % a, [P, X_GROUP * R], BF16, tag=tag)
            for i in range(X_GROUP):
                turned = ps.tile([P, LANES, P], F32, name="turned%d" % (X_GROUP * a + i))
                for j in range(LANES):
                    nc.tensor.transpose(turned[:, j, :], x_raw[a][:, i, j:R:LANES], ident[:])
                nc.scalar.copy(
                    grouped[:, i * R : (i + 1) * R].rearrange("p (m j) -> p m j", j=LANES),
                    turned[:].rearrange("p j m -> p m j"),
                )
            return grouped

        def quantise_x(a, grouped, tag):
            codes = tile("x_codes%d" % a, [P, X_GROUP * P], U32, tag=tag)
            scales = tile("x_scales%d" % a, [P, X_GROUP * P], U8)
            nc.vector.quantize_mx(out=codes[:].bitcast(E4M3), scales=scales[:], in_=grouped[:])
            return [(codes[:, i * P : (i + 1) * P], scales[:, i * P : (i + 1) * P]) for i in range(X_GROUP)]

        dw_tags = ("dw0", "dw1", "h_tab2", "inv2")

        def gather_h(t):
            if t == 0:
                h = tile("h0", [P, SLOTS], F32, tag="x_grouped0")
                nc.vector.tensor_copy(h[:], h_tab[0][:].indirect(offsets[:]))
                return h
            h = tile("h%d" % t, [P, SLOTS], F32, tag=dw_tags[t - 1])
            for cols in halves if t == X_GROUP else [slice(0, SLOTS)]:
                nc.scalar.activation(h[:, cols], h_tab[t][:].indirect(entries(cols)), ACT.Copy)
            return h

        def scaling(t, h):
            root = tile("root%d" % t, [P, SLOTS], F32)
            inv = tile("inv%d" % t, [P, SLOTS], F32)
            sign = tile("sign%d" % t, [P, SLOTS], F32)
            for cols in halves if t == X_GROUP else [slice(0, SLOTS)]:
                nc.scalar.activation(
                    root[:, cols], h[:, cols], ACT.Abs_reciprocal_sqrt, scale=1.0 / DECAY, bias=EPS / DECAY
                )
            nc.scalar.activation(sign[:], h[:], ACT.Sign, bias=EPS)
            nc.scalar.activation(inv[:], root[:], ACT.Square)
            return inv, sign

        g_codes = tile("g_codes", [P, SLOTS], U32)
        g_scales = tile("g_scales", [P, SLOTS], U8)
        g_grouped = []
        for a, cols in enumerate(halves):
            g_grouped.append(tile("g_grouped%d" % a, [P, HALF, LANES], BF16))
            nc.vector.tensor_copy(
                g_grouped[a][:].rearrange("p (c i) j -> p c j i", i=RUN),
                g_raw[:, :, cols].rearrange("p j (c i) -> p c j i", i=RUN),
            )
        x_mx = quantise_x(0, group_x(0, None), None)
        for a, cols in enumerate(halves):
            nc.vector.quantize_mx(
                out=g_codes[:, cols].bitcast(E5M2),
                scales=g_scales[:, cols],
                in_=g_grouped[a][:].rearrange("p w j -> p (w j)"),
            )

        def product(t):
            acc = ps.tile([P, SLOTS], F32, name="acc%d" % t)
            nc.tensor.matmul_mx(
                out=acc[:],
                lhsT=x_mx[t][0].bitcast(E4M3),
                lhsT_scale=x_mx[t][1],
                rhs=g_codes[:].bitcast(E5M2),
                rhs_scale=g_scales[:],
                start=True,
                stop=True,
            )
            return acc

        def copy_dw(t):
            dw = tile("dw%d" % t, [P, SLOTS], F32, tag=dw_tags[t])
            if t == X_GROUP:
                nc.scalar.activation(dw[:], accs[t][:], ACT.Copy, scale=1.0 / DECAY)
            else:
                nc.vector.tensor_scalar(dw[:], accs[t][:], 1.0 / DECAY, None, ALU.mult)
            return dw

        accs = [product(t) for t in range(X_GROUP)]
        scalings = [scaling(0, gather_h(0))]
        dws = [copy_dw(t) for t in range(X_GROUP)]

        def gather_m(t):
            total = tile("total%d" % t, [P, SLOTS], F32, tag="ratio%d" % (LAST - 1) if t == LAST else None)
            for cols in halves:
                nc.vector.tensor_tensor(total[:, cols], m_tab[t][:].indirect(entries(cols)), dws[t][:, cols], ALU.add)
            return total

        def scatter_nm(t, cols):
            win = nm_win[t % NM_WINDOWS]
            nc.scalar.activation(win[:].indirect(entries(cols)), totals[t][:, cols], ACT.Copy, scale=DECAY)
            return win

        def clipped_ratio(t):
            ratio = [tile("ratio%d%s" % (t, "a" * (1 - a)), [P, HALF], F32) for a in range(2)]
            for a, cols in enumerate(halves):
                nc.vector.tensor_tensor(ratio[a][:], totals[t][:, cols], scalings[t][0][:, cols], ALU.mult)
            cut = tile("cut%d" % t, [P, SLOTS], F32)
            for a, cols in enumerate(halves):
                nc.vector.tensor_scalar(cut[:, cols], ratio[a][:], 1.0, -1.0, ALU.min, ALU.max)
            return cut

        def scatter_up(t, cut):
            nc.vector.tensor_tensor(up_win[t][:].indirect(offsets[:]), cut[:], scalings[t][1][:], ALU.mult)
            nc.sync.dma_start(out=up_rows[t], in_=up_win[t][:])

        pairs_01 = tile("pairs_01", [P, 2, 2 * CHUNK, 2], BF16)
        pairs_2 = tile("pairs_2", [P, 2, PIECE, 2], BF16)
        pairs = [pairs_01[:, :, 0:CHUNK, :], pairs_01[:, :, CHUNK : 2 * CHUNK, :], pairs_2[:]]

        def round_up(copy, t, c):
            copy(pairs[c][:, t // 2, :, t % 2], up_win[t][:, c * CHUNK : min((c + 1) * CHUNK, FRONT)])

        def round_on_vector(t):
            for c in (0, 1, 2):
                round_up(nc.vector.tensor_copy, t, c)

        totals = [gather_m(0)]
        for t in range(LANES):
            scatter_nm(t, halves[0])
            cut = clipped_ratio(t)
            if t == 0:
                nm_win.append(window("nm_win2", nc.gpsimd, "ratio0"))
            if t == 1:
                x_mx.extend(quantise_x(1, late_x, "inv1"))
                accs.extend(product(s) for s in range(X_GROUP, LANES))
                up_win.append(window("up_win2", nc.gpsimd, "inv1"))
            if t == 2:
                dws.append(copy_dw(LAST))
                up_win.append(window("up_win3", nc.gpsimd, "ratio2a"))
            scatter_up(t, cut)
            if t < LAST:
                h_next = gather_h(t + 1)
                if t + 1 == X_GROUP:
                    dws.append(copy_dw(X_GROUP))
                totals.append(gather_m(t + 1))
            if t > 0:
                round_on_vector(t - 1)
            if t + 1 == X_GROUP:
                scalings.append(scaling(t + 1, h_next))
            nm_done = scatter_nm(t, halves[1])
            queue = nc.scalar if t == LAST else nc.sync
            queue.dma_start(out=nm_rows[t], in_=nm_done[:])
            if t < LAST and t + 1 != X_GROUP:
                scalings.append(scaling(t + 1, h_next))
            if t == 0:
                late_x = group_x(1, dw_tags[0])
        round_on_vector(LAST)

        late = tile("late", [P, 2 * BANKS * PIECE], BF16, tag="ratio%d" % (LAST - 1))
        woven = [tile("woven%d" % a, [P, CHUNK * LANES], BF16, tag="h_tab%d" % (a + 1))[:] for a in range(2)]
        woven.append(tile("woven2", [P, PIECE * LANES], BF16, tag="h_tab3")[:])
        ready = [woven[a // 2][:, a % 2 * PIECE * LANES : (a % 2 + 1) * PIECE * LANES] for a in range(FRONT // PIECE)]

        def weave(copy, word, c):
            copy(
                woven[c].bitcast(word).rearrange("p (c u) -> p c u", u=2),
                pairs[c].rearrange("p u c e -> p u (c e)").bitcast(word).rearrange("p u c -> p c u"),
            )

        back = [ps.tile([P, 2, 2, P], F32, name="back%d" % k, tag="acc%d" % k) for k in range(BANKS)]
        across = []
        for u in range(2):
            for k in range(BANKS):
                bank = ps.tile([P, 2, 2, P], F32, name="over%d%d" % (u, k), tag="turned%d" % k)
                for e in range(2):
                    for j in range(2):
                        at = FRONT + (2 * k + j) * P
                        nc.tensor.transpose(bank[:, j, e, :], up_win[2 * u + e][:, at : at + P], ident[:])
                if u == 0:
                    across.append(late[:, 2 * k * PIECE : 2 * (k + 1) * PIECE])
                else:
                    across.append(tile("across%d" % k, [P, 2 * PIECE], BF16)[:])
                nc.scalar.copy(
                    across[-1].rearrange("q (j p e) -> q j p e", j=2, e=2), bank[:].rearrange("q j e p -> q j p e")
                )
        for k in range(BANKS):
            for u in range(2):
                for j in range(2):
                    words = across[BANKS * u + k].bitcast(F32)
                    nc.tensor.transpose(back[k][:, j, u, :], words[:, j * P : (j + 1) * P], ident[:])
        for c in range(3):
            weave(nc.vector.tensor_copy, I32, c)
        for k in range(BANKS):
            ready.append(tile("ready%d" % k, [P, PIECE * LANES], BF16)[:])
            nc.scalar.copy(
                ready[-1].bitcast(F32).rearrange("p (j c u) -> p j c u", j=2, u=2),
                back[k][:].rearrange("p j u c -> p j c u"),
            )

        y_codes = tile("y_codes", [P, COLS], U32, tag="m_tab1")
        y_scales = tile("y_scales", [P, CHUNK], U8)
        piece = CHUNK // 2

        def store_words(cols):
            nc.sync.dma_start(
                out=out_2[0, :, cols, :].rearrange("p c l -> p (c l)").bitcast(I32), in_=y_codes[:, cols].bitcast(I32)
            )

        for c in range(CHUNKS):
            for a in range(2):
                cols = slice(c * CHUNK + a * piece, c * CHUNK + (a + 1) * piece)
                nc.vector.quantize_mx(
                    out=y_codes[:, cols].bitcast(E4M3),
                    scales=y_scales[LANES * c : P, a * piece : (a + 1) * piece],
                    in_=ready[2 * c + a],
                )
            store_words(slice(c * CHUNK, (c + 1) * CHUNK))
        for q in range(P // QUADRANT):
            nc.scalar.dma_start(
                out=out_3[0, LANES * q : LANES * (q + 1), :].rearrange("r (c x) -> c r x", c=CHUNKS).bitcast(I32),
                in_=y_scales[QUADRANT * q : QUADRANT * q + CHUNKS * LANES, :].bitcast(I32),
            )
